import numpy as np
CORES = [211,219,227,235,243,251,83,91,99,107,115,123]
N = 12
S, T = 8192, 512
def entries(a): return a.T.reshape(-1)
def pack(v, P): return np.ascontiguousarray(np.asarray(v, np.int32).reshape(-1, P).T)
def lists(rng, how):
    M = rng.integers(0, S, (N, S)); b = rng.integers(0, S, T)
    if how == "alike": M = np.stack([rng.permutation(S) for f in range(N)]); b[:] = rng.integers(S)
    if how == "edge":
        M = np.where(rng.random((N, S)) < 0.5, 0, S - 1); w = rng.permutation(N) % 2 * (S - 1); M[:, 0] = w; M[:, S - 1] = S - 1 - w
        b = np.where(rng.random(T) < 0.5, 0, S - 1); b[rng.permutation(T)[:2]] = [0, S - 1]
    if how == "fold":
        V = np.stack([rng.permutation(S)[:4] for f in range(N + 1)]); M = V[np.arange(N)[:, None], rng.integers(0, 4, (N, S))]
        M[np.arange(N)[:, None], V[1:]] = V[:N]; b[rng.permutation(T)[:4]] = V[N]
    if how == "mixed":
        k = np.concatenate([[3, 3], rng.permutation(np.arange(N - 2) % 3)])
        for f in range(N): M[f] = [np.arange(S), rng.permutation(S), M[f], rng.integers(0, S, 4)[rng.integers(0, 4, S)]][k[f]]
    if how == "turn": M = np.stack([rng.permutation(S) for f in range(N)]); b = rng.permutation(S)[:T]
    return {"bp": np.stack([pack(m, 16) for m in M]), "st": np.broadcast_to(pack(b, 16), (N, 16, T // 16)).copy()}
def setup_inputs(rng):
    return dict({"tab": rng.standard_normal((N, 128, S), dtype=np.float32)}, **lists(rng, "uniform"))
def setup_inputs_alike(rng):
    d = setup_inputs(rng); d.update(lists(rng, "alike"))
    for k in ("tab",): d[k] = (d[k].astype(np.float32) * 1048576.0).astype(d[k].dtype)
    return d
def setup_inputs_edge(rng):
    d = setup_inputs(rng); d.update(lists(rng, "edge"))
    for k in ("tab",): d[k] = (d[k].astype(np.float32) * (1 / 1024.0)).astype(d[k].dtype)
    return d
def setup_inputs_fold(rng):
    d = setup_inputs(rng); d.update(lists(rng, "fold"))
    return d
def setup_inputs_mixed(rng):
    d = setup_inputs(rng); d.update(lists(rng, "mixed"))
    return d
def setup_inputs_turn(rng):
    d = setup_inputs(rng); d.update(lists(rng, "turn"))
    return d
def check_inputs(x):
    bad = []
    if x["bp"].min() < 0 or x["bp"].max() >= S: bad.append("bp out of range")
    if x["st"].min() < 0 or x["st"].max() >= S: bad.append("st out of range")
    if not all(np.array_equal(a, x["st"][0]) for a in x["st"]): bad.append("st isn't alike on all ranks")
    return bad
def reference(tab, bp, st):
    b = entries(st[0]); y = np.zeros((N, 128, T), tab.dtype)
    for f in range(N - 1, -1, -1):
        y[f] = tab[f][:, b]
        b = entries(bp[f])[b]
    return {"y": y}

@@ -1,0 +1,318 @@
+from concourse.bass import DstId, RemoteDMATransfer
+from concourse.mybir import AluOpType, ActivationFunctionType
+
+N = 12
+NW = 4
+EB = 128
+CB = EB // 16
+BATCHES = [[1, 2, 3, 4], [5, 6, 7], [8, 9], [10], [11]]
+LAST = N - 1
+BIG = 16384.0
+
+SCRATCH = {
+    "raw": ("sbuf", [128, 512], "int32"),
+    "two": ("sbuf", [128, 128], "int32"),
+    "tb": ("sbuf", [128, 128], "bfloat16"),
+    "st8": ("sbuf", [128, 32], "int32"),
+    "off": ("sbuf", [128, 32], "uint16"),
+    "win": ("sbuf", [128, 8192], "float32"),
+    "yy": ("sbuf", [128, 512], "float32"),
+    "s4": ("sbuf", [128, 4], "int32"),
+    "tbl": ("sbuf", [128, N * 128], "bfloat16"),
+    "ci": ("sbuf", [128, 8], "int32"),
+    "cf": ("sbuf", [128, 8], "float32"),
+    "rr": ("sbuf", [128, 4, 64], "bfloat16"),
+    "sel": ("sbuf", [128, 2, 16], "bfloat16"),
+    "one": ("sbuf", [128, 128], "bfloat16"),
+    "nul": ("sbuf", [128, 128], "bfloat16"),
+    "ly": ("sbuf", [128, 128], "bfloat16"),
+    "lx": ("sbuf", [128, 128], "bfloat16"),
+    "lf": ("sbuf", [128, 128], "bfloat16"),
+    "e16": ("sbuf", [16, 128], "bfloat16"),
+    "bt": ("sbuf", [16, 128], "bfloat16"),
+    "rs": ("sbuf", [128, 128], "float32"),
+    "yc": ("sbuf", [128, 1], "float32"),
+    "xc": ("sbuf", [128, 1], "float32"),
+    "ohA": ("sbuf", [128, 64], "bfloat16"),
+    "ohB": ("sbuf", [128, 64], "bfloat16"),
+    "mxA": ("sbuf", [128, 64], "bfloat16"),
+    "mxB": ("sbuf", [128, 64], "bfloat16"),
+    "z0": ("sbuf", [128, 128], "bfloat16"),
+    "z1": ("sbuf", [128, 128], "bfloat16"),
+    "sc": ("sbuf", [128, LAST * 128], "float32"),
+    "offo": ("sbuf", [128, LAST * CB], "uint16"),
+    "ptA": ("psum", [128, 512], "float32"),
+    "ptB": ("psum", [128, 512], "float32"),
+    "pyA": ("psum", [128, 512], "float32"),
+    "pyB": ("psum", [128, 512], "float32"),
+    "pxA": ("psum", [128, 512], "float32"),
+    "pxB": ("psum", [128, 512], "float32"),
+    "po0": ("psum", [128, 512], "float32"),
+    "po1": ("psum", [128, 512], "float32"),
+}
+SEMAPHORES = (["ld", "prep", "left", "offin", "tabin", "stin", "st8in", "offok", "yv", "ya", "ys",
+               "cst", "gcs", "ini", "pO", "vS0", "vS1", "gone"]
+              + [k + h for k in ("pT", "pY", "pX", "vZ", "vY", "vX") for h in "AB"]
+              + ["m%d" % f for f in range(1, N)] + ["cp%d" % b for b in range(len(BATCHES))])
+
+
+def _bits(mask):
+    return [1 << e for e in range(16) if (mask >> e) & 1]
+
+
+def _split(mask, n):
+    e = _bits(mask)
+    if n == 1:
+        sizes = [len(e)]
+    elif n == 2:
+        sizes = [len(e) // 2] * 2
+    elif n == 3:
+        sizes = [len(e) // 4, len(e) // 4, len(e) // 2]
+    else:
+        sizes = [len(e) // 4] * 4
+    out, at = [], 0
+    for s in sizes:
+        out.append(sum(e[at:at + s]))
+        at += s
+    return out
+
+
+def _workers(cores, topo):
+    def at(c):
+        return (topo.host(c), topo.chip(c))
+    used = {at(c) for c in cores}
+    got = {True: [], False: []}
+    for c in range(256):
+        if at(c) in used or topo.die(c) != topo.die(cores[0]):
+            continue
+        if not all(topo.may_write(c, d) and topo.may_write(d, c) for d in cores):
+            continue
+        k = topo.same_plane(c, cores[0])
+        if len(got[k]) < NW // 2:
+            got[k].append(c)
+            used.add(at(c))
+    return got[True] + got[False]
+
+
+def _common(srcs_dsts, topo):
+    m = 0xFFFF
+    for s, d in srcs_dsts:
+        m &= topo.mask(s, d)
+    return m
+
+
+def _dst(d, core, topo):
+    rid, pid = topo.addr(d, core)
+    return DstId(rid=rid, pnc=pid)
+
+
+def rank_program(g, core, T, topo):
+    cores = list(T.cores)
+    workers = _workers(cores, topo)
+    rank = T.rank_of(core)
+    if rank is not None:
+        _rank(g, core, rank, cores, workers, T, topo)
+    elif core in workers:
+        _worker(g, core, workers.index(core), cores, T, topo)
+
+
+def _rank(g, core, f, cores, workers, T, topo):
+    v, act, sync, S = g.vector, g.scalar, g.sync, T.sem
+    send_mask = _common([(core, w) for w in workers], topo)
+    ne = len(_bits(send_mask))
+    W0 = 2048
+
+    if f > 0:
+        for b in range(8):
+            q = sync if b % 2 == 0 else act
+            q.dma_start(out=T.raw[16 * b:16 * b + 16, 0:505], in_=T.bp[:, b:b + 505]).then_inc(S.ld, 16)
+    else:
+        sync.dma_start(out=T.s4[:], in_=T.st[:]).then_inc(S.ld, 16)
+    sync.dma_start(out=T.win[:, 0:W0], in_=T.tab[:, 0:W0]).then_inc(S.tabin, 16)
+
+    if f > 0:
+        v.wait_ge(S.ld, 128)
+        v.tensor_scalar(out=T.two[:, 0:64], in0=T.raw[:, 0:505:8], scalar1=7, scalar2=None,
+                        op0=AluOpType.logical_shift_right).then_inc(S.prep, 1)
+        v.tensor_scalar(out=T.two[:, 64:128], in0=T.raw[:, 0:505:8], scalar1=127, scalar2=None,
+                        op0=AluOpType.bitwise_and).then_inc(S.prep, 1)
+        v.wait_ge(S.prep, 2)
+        v.tensor_copy(out=T.tb[:], in_=T.two[:]).then_inc(S.prep, 1)
+        g.wait_ge(S.prep, 3)
+        src, dst, sem = T.tb[:], T.tbl[:, 128 * f:128 * f + 128], S["m%d" % f]
+    else:
+        g.wait_ge(S.ld, 16)
+        src, dst, sem = T.s4[:], T.s4[:], S.stin
+    g.remote_dma_fused([RemoteDMATransfer(dst_ids=[_dst(w, core, topo) for w in workers], dma_engine_mask=send_mask,
+                                          remote_sem=sem, srcs=[src], dsts=[dst for w in workers])],
+                       local_sem=S.left)
+
+    sync.wait_ge(S.left, ne)
+    n = 16
+    for c in range(W0, 8192, 2048):
+        sync.dma_start(out=T.win[:, c:c + 2048], in_=T.tab[:, c:c + 2048]).then_inc(S.tabin, 16)
+        n += 16
+
+    if f == LAST:
+        for b in range(8):
+            act.dma_start(out=T.st8[16 * b:16 * b + 16, :], in_=T.st[:]).then_inc(S.st8in, 16)
+        v.wait_ge(S.st8in, 128)
+        v.tensor_copy(out=T.off[:], in_=T.st8[:]).then_inc(S.offok, 1)
+        osem, on = S.offok, 1
+    else:
+        osem, on = S.offin, 0
+        for w in workers:
+            for b in BATCHES:
+                if LAST - f in b:
+                    m = _common([(w, cores[LAST - t]) for t in b], topo)
+                    on += len(_bits(_split(m, len(b))[b.index(LAST - f)]))
+    v.wait_ge(S.tabin, n)
+    v.wait_ge(osem, on)
+    v.tensor_copy(out=T.yy[:, 0:256], in_=T.win[:].indirect(T.off[:, 0:16])).then_inc(S.yv, 1)
+    act.wait_ge(S.tabin, n)
+    act.wait_ge(osem, on)
+    act.activation(out=T.yy[:, 256:512], in_=T.win[:].indirect(T.off[:, 16:32]),
+                   func=ActivationFunctionType.Copy, bias=-0.0).then_inc(S.ya, 1)
+    sync.wait_ge(S.yv, 1)
+    sync.dma_start(out=T.y[:, 0:256], in_=T.yy[:, 0:256]).then_inc(S.ys, 16)
+    act.wait_ge(S.ya, 1)
+    act.dma_start(out=T.y[:, 256:512], in_=T.yy[:, 256:512]).then_inc(S.ys, 16)
+    sync.wait_ge(S.ys, 32)
+
+
+def _worker(g, core, r, cores, T, topo):
+    v, pe, S = g.vector, g.tensor, T.sem
+    H = "AB"
+    eq, mult, add = AluOpType.is_equal, AluOpType.mult, AluOpType.add
+
+    fills = [(T.one[:], 1.0), (T.nul[:], 0.0), (T.rs[:], 0.0),
+             (T.lx[0:64, :], 1.0), (T.lx[64:128, :], 0.0),
+             (T.ly[0:64, :], 0.0), (T.ly[64:128, :], 1.0),
+             (T.lf[0:64, :], 128.0), (T.lf[64:128, :], 1.0)]
+    for ap, c in fills:
+        v.memset(ap, c).then_inc(S.cst, 1)
+    v.wait_ge(S.cst, len(fills))
+    v.memset(T.rs[:, 0:128:16], -2 * BIG).then_inc(S.cst, 1)
+    ncst = len(fills) + 1
+    made = [lambda: g.iota(T.yc[:], [[0, 1]], 0, 1, allow_small_or_imprecise_dtypes=True),
+            lambda: g.iota(T.xc[0:64, :], [[0, 1]], 0, 1, allow_small_or_imprecise_dtypes=True),
+            lambda: g.iota(T.xc[64:128, :], [[0, 1]], 0, 1, allow_small_or_imprecise_dtypes=True),
+            lambda: g.affine_select(T.sel[:, 0, :], T.one[:, 0:16], [[8, 16]], eq, 0.0, 2 * r, -1),
+            lambda: g.affine_select(T.sel[:, 1, :], T.one[:, 0:16], [[8, 16]], eq, 0.0, 2 * r + 1, -1),
+            lambda: g.affine_select(T.e16[:], T.one[0:16, :], [[0, 8], [1, 16]], eq, 0.0, 0, -1),
+            lambda: g.affine_select(T.bt[:], T.nul[0:16, :], [[0, 8], [1, 16]], eq, -BIG, 0, -1)]
+    g.wait_ge(S.cst, ncst)
+    for k, make in enumerate(made):
+        if k:
+            g.wait_ge(S.gcs, k)
+        make().then_inc(S.gcs, 1)
+    ngcs = len(made)
+
+    v.wait_ge(S.cst, ncst)
+    v.wait_ge(S.gcs, ngcs)
+    pe.wait_ge(S.cst, ncst)
+    pe.wait_ge(S.gcs, ngcs)
+    ns = len(_bits(_common([(cores[0], core)], topo)))
+    v.wait_ge(S.stin, ns)
+    v.tensor_scalar(out=T.ci[:, 0:4], in0=T.s4[:], scalar1=7, scalar2=None,
+                    op0=AluOpType.logical_shift_right).then_inc(S.ini, 1)
+    v.tensor_scalar(out=T.ci[:, 4:8], in0=T.s4[:], scalar1=127, scalar2=None,
+                    op0=AluOpType.bitwise_and).then_inc(S.ini, 1)
+    v.wait_ge(S.ini, 2)
+    v.tensor_copy(out=T.cf[:], in_=T.ci[:]).then_inc(S.ini, 1)
+    v.wait_ge(S.ini, 3)
+    for k in range(2):
+        for l in range(4):
+            v.tensor_scalar(out=T.rr[:, 2 * k:2 * k + 2, 16 * l:16 * l + 16], in0=T.sel[:],
+                            scalar1=T.cf[:, 4 * k + l:4 * k + l + 1], scalar2=None, op0=mult).then_inc(S.ini, 1)
+    pe.wait_ge(S.ini, 11)
+    for a, h in enumerate(H):
+        pe.matmul(T["py" + h][:, 0:64], T.one[:], T.rr[:, 2 + a, :], True, True).then_inc(S["pY" + h], 1)
+        pe.matmul(T["px" + h][:, 0:64], T.one[:], T.rr[:, a, :], True, True).then_inc(S["pX" + h], 1)
+
+    def onehots(h, n):
+        v.wait_ge(S["pY" + h], n)
+        v.tensor_scalar(out=T["oh" + h][:], in0=T["py" + h][:, 0:64], scalar1=T.yc[:, 0:1], scalar2=None,
+                        op0=eq).then_inc(S["vY" + h], 1)
+        v.wait_ge(S["pX" + h], n)
+        v.tensor_scalar(out=T["mx" + h][:], in0=T["px" + h][:, 0:64], scalar1=T.xc[:, 0:1], scalar2=None,
+                        op0=eq).then_inc(S["vX" + h], 1)
+
+    nscan = [0, 0]
+
+    def scan(t):
+        v.wait_ge(S.pO, t)
+        v.tensor_tensor_scan(T.sc[:, 128 * (t - 1):128 * t], T.rs[:], T["po%d" % (t % 2)][:, 0:128], 0.0,
+                             add, AluOpType.max).then_inc(S["vS%d" % (t % 2)], 1)
+        nscan[t % 2] += 1
+
+    def pack(t):
+        for b, steps in enumerate(BATCHES):
+            if steps[-1] == t:
+                for k in range(2):
+                    if nscan[k]:
+                        v.wait_ge(S["vS%d" % k], nscan[k])
+                t0 = steps[0] - 1
+                v.tensor_copy(out=T.offo[:, CB * t0:CB * t],
+                              in_=T.sc[:, 128 * t0 + 15:128 * t:16]).then_inc(S["cp%d" % b], 1)
+
+    def base(t):
+        k = t % 2
+        before = len([u for u in range(1, t) if u % 2 == k])
+        if before:
+            pe.wait_ge(S["vS%d" % k], before)
+        pe.matmul(T["po%d" % k][:, 0:128], T.e16[:], T.bt[:], True, False)
+
+    def states(t):
+        pe.matmul(T["po%d" % (t % 2)][:, 0:128], T.lf[:], T["z%d" % (t % 2)][:], False, True).then_inc(S.pO, 1)
+
+    for h in H:
+        onehots(h, 1)
+    for t in range(1, N):
+        f = N - t
+        z = T["z%d" % (t % 2)]
+        pe.wait_ge(S["m%d" % f], len(_bits(_common([(cores[f], core)], topo))))
+        for h in H:
+            pe.wait_ge(S["vY" + h], t)
+            pe.matmul(T["pt" + h][:, 0:64], T.tbl[:, 128 * f:128 * f + 128], T["oh" + h][:], True,
+                      True).then_inc(S["pT" + h], 1)
+        if t > 1:
+            states(t - 1)
+        if t == LAST:
+            base(t)
+        for a, h in enumerate(H):
+            pe.wait_ge(S["vZ" + h], t)
+            if t < LAST:
+                zh = z[:, 64 * a:64 * a + 64]
+                pe.matmul(T["py" + h][:, 0:64], T.ly[:], zh, True, True).then_inc(S["pY" + h], 1)
+                pe.matmul(T["px" + h][:, 0:64], T.lx[:], zh, True, True).then_inc(S["pX" + h], 1)
+        if t < LAST:
+            base(t)
+        else:
+            states(t)
+        for a, h in enumerate(H):
+            v.wait_ge(S["vX" + h], t)
+            v.wait_ge(S["pT" + h], t)
+            v.tensor_tensor(out=z[:, 64 * a:64 * a + 64], in0=T["pt" + h][:, 0:64], in1=T["mx" + h][:],
+                            op=mult).then_inc(S["vZ" + h], 1)
+        if t > 1:
+            scan(t - 1)
+        if t < LAST:
+            onehots("A", t + 1)
+            pack(t - 1)
+            onehots("B", t + 1)
+        else:
+            pack(t - 1)
+            scan(t)
+            pack(t)
+
+    total = 0
+    for b, steps in enumerate(BATCHES):
+        m = _common([(core, cores[LAST - t]) for t in steps], topo)
+        g.wait_ge(S["cp%d" % b], 1)
+        g.remote_dma_fused([RemoteDMATransfer(dst_ids=[_dst(cores[LAST - t], core, topo)], dma_engine_mask=mm,
+                                              remote_sem=S.offin, srcs=[T.offo[:, CB * (t - 1):CB * t]],
+                                              dsts=[T.off[:, CB * r:CB * r + CB]])
+                            for t, mm in zip(steps, _split(m, len(steps)))], local_sem=S.gone)
+        total += len(_bits(m))
+    g.wait_ge(S.gone, total)

@@ -5,42 +5,56 @@ N = 12
 NW = 4
 EB = 128
 CB = EB // 16
-BATCHES = [[1, 2, 3, 4], [5, 6, 7], [8, 9], [10], [11]]
 LAST = N - 1
+NT = N - 2
+LISTER = 2
+BATCHES = [[1, 2, 3, 4], [5, 6], [7, 8], [9], [10]]
+FIRST = {11: 0, 10: 512, 9: 1024, 8: 1024, 7: 1536, 6: 1536, 5: 2048, 4: 2048, 3: 2048, 2: 2048, 1: 0, 0: 8192}
 BIG = 16384.0
+MX, MY = 0x11F0, 0x0E0F
+SH = 2048
 
 SCRATCH = {
-    "raw": ("sbuf", [128, 512], "int32"),
+    "raw": ("sbuf", [128, 64], "int32"),
+    "raw8": ("sbuf", [128, 512], "int32"),
+    "of1s": ("sbuf", [128, 512], "uint16"),
+    "of1": ("sbuf", [128, 512], "uint16"),
     "two": ("sbuf", [128, 128], "int32"),
-    "tb": ("sbuf", [128, 128], "bfloat16"),
+    "tb": ("sbuf", [128, 128], "float16"),
     "st8": ("sbuf", [128, 32], "int32"),
     "off": ("sbuf", [128, 32], "uint16"),
     "win": ("sbuf", [128, 8192], "float32"),
+    "win1": ("sbuf", [128, 8192], "float32"),
     "yy": ("sbuf", [128, 512], "float32"),
     "s4": ("sbuf", [128, 4], "int32"),
-    "tbl": ("sbuf", [128, N * 128], "bfloat16"),
+    "tbl": ("sbuf", [128, N * 128], "float16"),
+    "ip": ("sbuf", [128, 1], "int32"),
+    "ic": ("sbuf", [128, 4], "int32"),
+    "fc": ("sbuf", [128, 4], "float32"),
     "ci": ("sbuf", [128, 8], "int32"),
     "cf": ("sbuf", [128, 8], "float32"),
-    "rr": ("sbuf", [128, 4, 64], "bfloat16"),
+    "rr": ("sbuf", [128, 4, 64], "float16"),
     "sel": ("sbuf", [128, 2, 16], "bfloat16"),
-    "one": ("sbuf", [128, 128], "bfloat16"),
+    "onb": ("sbuf", [128, 128], "bfloat16"),
     "nul": ("sbuf", [128, 128], "bfloat16"),
-    "ly": ("sbuf", [128, 128], "bfloat16"),
-    "lx": ("sbuf", [128, 128], "bfloat16"),
-    "lf": ("sbuf", [128, 128], "bfloat16"),
+    "lyb": ("sbuf", [128, 128], "bfloat16"),
+    "lxb": ("sbuf", [128, 128], "bfloat16"),
+    "one": ("sbuf", [128, 128], "float16"),
+    "ly": ("sbuf", [128, 128], "float16"),
+    "lx": ("sbuf", [128, 128], "float16"),
     "e16": ("sbuf", [16, 128], "bfloat16"),
     "bt": ("sbuf", [16, 128], "bfloat16"),
     "rs": ("sbuf", [128, 128], "float32"),
     "yc": ("sbuf", [128, 1], "float32"),
     "xc": ("sbuf", [128, 1], "float32"),
-    "ohA": ("sbuf", [128, 64], "bfloat16"),
-    "ohB": ("sbuf", [128, 64], "bfloat16"),
-    "mxA": ("sbuf", [128, 64], "bfloat16"),
-    "mxB": ("sbuf", [128, 64], "bfloat16"),
-    "z0": ("sbuf", [128, 128], "bfloat16"),
-    "z1": ("sbuf", [128, 128], "bfloat16"),
-    "sc": ("sbuf", [128, LAST * 128], "float32"),
-    "offo": ("sbuf", [128, LAST * CB], "uint16"),
+    "ohA": ("sbuf", [128, 64], "float16"),
+    "ohB": ("sbuf", [128, 64], "float16"),
+    "mxA": ("sbuf", [128, 64], "float16"),
+    "mxB": ("sbuf", [128, 64], "float16"),
+    "z0": ("sbuf", [128, 128], "float16"),
+    "z1": ("sbuf", [128, 128], "float16"),
+    "sc": ("sbuf", [128, NT * 128], "float32"),
+    "offo": ("sbuf", [128, NT * CB], "uint16"),
     "ptA": ("psum", [128, 512], "float32"),
     "ptB": ("psum", [128, 512], "float32"),
     "pyA": ("psum", [128, 512], "float32"),
@@ -50,8 +64,9 @@ SCRATCH = {
     "po0": ("psum", [128, 512], "float32"),
     "po1": ("psum", [128, 512], "float32"),
 }
-SEMAPHORES = (["ld", "prep", "left", "offin", "tabin", "stin", "st8in", "offok", "yv", "ya", "ys",
-               "cst", "gcs", "ini", "pO", "vS0", "vS1", "gone"]
+SEMAPHORES = (["ld", "ls", "prep", "left", "leftl", "offin", "tab0", "tabin", "stin", "st8in", "offok", "comp", "yv", "ya",
+               "ys", "cbf", "cst", "chf", "cip", "csel", "cbase", "cc1", "cc2", "cc3", "ini", "iniY", "iniX", "pO", "vS0",
+               "vS1", "vL", "gone"]
               + [k + h for k in ("pT", "pY", "pX", "vZ", "vY", "vX") for h in "AB"]
               + ["m%d" % f for f in range(1, N)] + ["cp%d" % b for b in range(len(BATCHES))])
 
@@ -62,19 +77,8 @@ def _bits(mask):
 
 def _split(mask, n):
     e = _bits(mask)
-    if n == 1:
-        sizes = [len(e)]
-    elif n == 2:
-        sizes = [len(e) // 2] * 2
-    elif n == 3:
-        sizes = [len(e) // 4, len(e) // 4, len(e) // 2]
-    else:
-        sizes = [len(e) // 4] * 4
-    out, at = [], 0
-    for s in sizes:
-        out.append(sum(e[at:at + s]))
-        at += s
-    return out
+    k = len(e) // n
+    return [sum(e[k * i:k * i + k]) for i in range(n)]
 
 
 def _workers(cores, topo):
@@ -106,6 +110,15 @@ def _dst(d, core, topo):
     return DstId(rid=rid, pnc=pid)
 
 
+def _takers(t):
+    return [LAST - t] if t < NT else [LAST - t, 0]
+
+
+def _batch_masks(b, w, cores, topo):
+    m = _common([(w, cores[f]) for t in BATCHES[b] for f in _takers(t)], topo)
+    return _split(m, len(BATCHES[b]))
+
+
 def rank_program(g, core, T, topo):
     cores = list(T.cores)
     workers = _workers(cores, topo)
@@ -118,40 +131,58 @@ def rank_program(g, core, T, topo):
 
 def _rank(g, core, f, cores, workers, T, topo):
     v, act, sync, S = g.vector, g.scalar, g.sync, T.sem
-    send_mask = _common([(core, w) for w in workers], topo)
-    ne = len(_bits(send_mask))
-    W0 = 2048
+    first = FIRST[f]
 
-    if f > 0:
+    def send(src, dst, to, sem, left):
+        mask = _common([(core, c) for c in to], topo)
+        g.remote_dma_fused([RemoteDMATransfer(dst_ids=[_dst(c, core, topo) for c in to], dma_engine_mask=mask,
+                                              remote_sem=sem, srcs=[src], dsts=[dst for c in to])], local_sem=left)
+        return len(_bits(mask))
+
+    if f == LISTER:
+        sync.dma_start(out=T.s4[:], in_=T.st[:]).then_inc(S.ls, 16)
+    if f > 1:
+        for a, q in enumerate((sync, act)):
+            q.dma_start(out=T.raw[:, 32 * a:32 * a + 32], in_=T.bp[:, 256 * a:256 * a + 256]).then_inc(S.ld, 16)
+    elif f == 1:
         for b in range(8):
             q = sync if b % 2 == 0 else act
-            q.dma_start(out=T.raw[16 * b:16 * b + 16, 0:505], in_=T.bp[:, b:b + 505]).then_inc(S.ld, 16)
-    else:
-        sync.dma_start(out=T.s4[:], in_=T.st[:]).then_inc(S.ld, 16)
-    sync.dma_start(out=T.win[:, 0:W0], in_=T.tab[:, 0:W0]).then_inc(S.tabin, 16)
+            q.dma_start(out=T.raw8[16 * b:16 * b + 16, :], in_=T.bp[:]).then_inc(S.ld, 16)
+    if f == LISTER:
+        g.wait_ge(S.ls, 16)
+        nl = send(T.s4[:], T.s4[:], workers, S.stin, S.leftl)
+        sync.wait_ge(S.leftl, nl)
+    if first:
+        sync.dma_start(out=T.win[:, 0:first], in_=T.tab[:, 0:first]).then_inc(S.tab0, 16)
 
-    if f > 0:
-        v.wait_ge(S.ld, 128)
-        v.tensor_scalar(out=T.two[:, 0:64], in0=T.raw[:, 0:505:8], scalar1=7, scalar2=None,
-                        op0=AluOpType.logical_shift_right).then_inc(S.prep, 1)
-        v.tensor_scalar(out=T.two[:, 64:128], in0=T.raw[:, 0:505:8], scalar1=127, scalar2=None,
+    if f > 1:
+        v.wait_ge(S.ld, 32)
+        v.tensor_scalar(out=T.two[:, 0:64], in0=T.raw[:], scalar1=MX, scalar2=None,
+                        op0=AluOpType.bitwise_and).then_inc(S.prep, 1)
+        v.tensor_scalar(out=T.two[:, 64:128], in0=T.raw[:], scalar1=MY, scalar2=None,
                         op0=AluOpType.bitwise_and).then_inc(S.prep, 1)
         v.wait_ge(S.prep, 2)
-        v.tensor_copy(out=T.tb[:], in_=T.two[:]).then_inc(S.prep, 1)
+        v.tensor_scalar(out=T.tb[:], in0=T.two[:], scalar1=-float(SH), scalar2=None,
+                        op0=AluOpType.add).then_inc(S.prep, 1)
         g.wait_ge(S.prep, 3)
-        src, dst, sem = T.tb[:], T.tbl[:, 128 * f:128 * f + 128], S["m%d" % f]
-    else:
-        g.wait_ge(S.ld, 16)
-        src, dst, sem = T.s4[:], T.s4[:], S.stin
-    g.remote_dma_fused([RemoteDMATransfer(dst_ids=[_dst(w, core, topo) for w in workers], dma_engine_mask=send_mask,
-                                          remote_sem=sem, srcs=[src], dsts=[dst for w in workers])],
-                       local_sem=S.left)
+        if first:
+            g.wait_ge(S.tab0, 16)
+        ne = send(T.tb[:], T.tbl[:, 128 * f:128 * f + 128], workers, S["m%d" % f], S.left)
+    elif f == 1:
+        v.wait_ge(S.ld, 128)
+        v.tensor_copy(out=T.of1s[:], in_=T.raw8[:]).then_inc(S.prep, 1)
+        g.wait_ge(S.prep, 1)
+        ne = send(T.of1s[:], T.of1[:], [cores[0]], S.m1, S.left)
 
-    sync.wait_ge(S.left, ne)
-    n = 16
-    for c in range(W0, 8192, 2048):
-        sync.dma_start(out=T.win[:, c:c + 2048], in_=T.tab[:, c:c + 2048]).then_inc(S.tabin, 16)
-        n += 16
+    if first < 8192:
+        sync.wait_ge(S.left, ne)
+        sync.dma_start(out=T.win[:, first:8192], in_=T.tab[:, first:8192]).then_inc(S.tabin, 16)
+
+    def tab_there(q):
+        if first:
+            q.wait_ge(S.tab0, 16)
+        if first < 8192:
+            q.wait_ge(S.tabin, 16)
 
     if f == LAST:
         for b in range(8):
@@ -162,16 +193,28 @@ def _rank(g, core, f, cores, workers, T, topo):
     else:
         osem, on = S.offin, 0
         for w in workers:
-            for b in BATCHES:
-                if LAST - f in b:
-                    m = _common([(w, cores[LAST - t]) for t in b], topo)
-                    on += len(_bits(_split(m, len(b))[b.index(LAST - f)]))
-    v.wait_ge(S.tabin, n)
+            for b, steps in enumerate(BATCHES):
+                for t, mm in zip(steps, _batch_masks(b, w, cores, topo)):
+                    if f in _takers(t):
+                        on += len(_bits(mm))
+
+    win = T.win
+    tab_there(v)
+    tab_there(act)
+    if f == 0:
+        n1 = len(_bits(_common([(cores[1], core)], topo)))
+        win = T.win1
+        v.wait_ge(S.m1, n1)
+        v.tensor_copy(out=win[:, 0:4096], in_=T.win[:].indirect(T.of1[:, 0:256])).then_inc(S.comp, 1)
+        act.wait_ge(S.m1, n1)
+        act.activation(out=win[:, 4096:8192], in_=T.win[:].indirect(T.of1[:, 256:512]),
+                       func=ActivationFunctionType.Copy, bias=-0.0).then_inc(S.comp, 1)
+        v.wait_ge(S.comp, 2)
+        act.wait_ge(S.comp, 2)
     v.wait_ge(osem, on)
-    v.tensor_copy(out=T.yy[:, 0:256], in_=T.win[:].indirect(T.off[:, 0:16])).then_inc(S.yv, 1)
-    act.wait_ge(S.tabin, n)
+    v.tensor_copy(out=T.yy[:, 0:256], in_=win[:].indirect(T.off[:, 0:16])).then_inc(S.yv, 1)
     act.wait_ge(osem, on)
-    act.activation(out=T.yy[:, 256:512], in_=T.win[:].indirect(T.off[:, 16:32]),
+    act.activation(out=T.yy[:, 256:512], in_=win[:].indirect(T.off[:, 16:32]),
                    func=ActivationFunctionType.Copy, bias=-0.0).then_inc(S.ya, 1)
     sync.wait_ge(S.yv, 1)
     sync.dma_start(out=T.y[:, 0:256], in_=T.yy[:, 0:256]).then_inc(S.ys, 16)
@@ -184,50 +227,59 @@ def _worker(g, core, r, cores, T, topo):
     v, pe, S = g.vector, g.tensor, T.sem
     H = "AB"
     eq, mult, add = AluOpType.is_equal, AluOpType.mult, AluOpType.add
+    band, shr = AluOpType.bitwise_and, AluOpType.logical_shift_right
 
-    fills = [(T.one[:], 1.0), (T.nul[:], 0.0), (T.rs[:], 0.0),
-             (T.lx[0:64, :], 1.0), (T.lx[64:128, :], 0.0),
-             (T.ly[0:64, :], 0.0), (T.ly[64:128, :], 1.0),
-             (T.lf[0:64, :], 128.0), (T.lf[64:128, :], 1.0)]
+    g.iota(T.ip[:], [[0, 1]], 0, 1).then_inc(S.cip, 1)
+    v.memset(T.onb[:], 1.0).then_inc(S.cbf, 1)
+    v.memset(T.nul[:], 2.0 * SH).then_inc(S.cbf, 1)
+    g.wait_ge(S.cbf, 2)
+    g.affine_select(T.sel[:, 0, :], T.onb[:, 0:16], [[8, 16]], eq, 0.0, 2 * r, -1).then_inc(S.csel, 1)
+    g.affine_select(T.sel[:, 1, :], T.onb[:, 0:16], [[8, 16]], eq, 0.0, 2 * r + 1, -1).then_inc(S.csel, 1)
+    g.affine_select(T.e16[:], T.onb[0:16, :], [[0, 8], [1, 16]], eq, 0.0, 0, -1).then_inc(S.cbase, 1)
+    g.affine_select(T.bt[:], T.nul[0:16, :], [[0, 8], [1, 16]], eq, -BIG, 0, -1).then_inc(S.cbase, 1)
+
+    fills = [(T.rs[:], 0.0),
+             (T.lxb[0:64, :], 1.0), (T.lxb[64:128, :], 0.0),
+             (T.lyb[0:64, :], 0.0), (T.lyb[64:128, :], 1.0)]
     for ap, c in fills:
         v.memset(ap, c).then_inc(S.cst, 1)
+    v.wait_ge(S.cip, 1)
+    for k, (op, c) in enumerate(((shr, 3), (band, 7), (band, 31), (band, 32))):
+        v.tensor_scalar(out=T.ic[:, k:k + 1], in0=T.ip[:], scalar1=c, scalar2=None, op0=op).then_inc(S.cc1, 1)
+    v.wait_ge(S.cc1, 4)
+    for k, (m, a) in enumerate(((1.0, 0.0), (512.0, -float(SH)), (16.0, -float(SH)), (128.0, 0.0))):
+        v.tensor_scalar(out=T.fc[:, k:k + 1], in0=T.ic[:, k:k + 1], scalar1=m, scalar2=a, op0=mult,
+                        op1=add).then_inc(S.cc2, 1)
+    v.wait_ge(S.cc2, 4)
+    v.tensor_tensor(out=T.yc[:], in0=T.fc[:, 0:1], in1=T.fc[:, 1:2], op=add).then_inc(S.cc3, 1)
+    v.tensor_tensor(out=T.xc[:], in0=T.fc[:, 2:3], in1=T.fc[:, 3:4], op=add).then_inc(S.cc3, 1)
+    v.wait_ge(S.cbf, 2)
     v.wait_ge(S.cst, len(fills))
-    v.memset(T.rs[:, 0:128:16], -2 * BIG).then_inc(S.cst, 1)
-    ncst = len(fills) + 1
-    made = [lambda: g.iota(T.yc[:], [[0, 1]], 0, 1, allow_small_or_imprecise_dtypes=True),
-            lambda: g.iota(T.xc[0:64, :], [[0, 1]], 0, 1, allow_small_or_imprecise_dtypes=True),
-            lambda: g.iota(T.xc[64:128, :], [[0, 1]], 0, 1, allow_small_or_imprecise_dtypes=True),
-            lambda: g.affine_select(T.sel[:, 0, :], T.one[:, 0:16], [[8, 16]], eq, 0.0, 2 * r, -1),
-            lambda: g.affine_select(T.sel[:, 1, :], T.one[:, 0:16], [[8, 16]], eq, 0.0, 2 * r + 1, -1),
-            lambda: g.affine_select(T.e16[:], T.one[0:16, :], [[0, 8], [1, 16]], eq, 0.0, 0, -1),
-            lambda: g.affine_select(T.bt[:], T.nul[0:16, :], [[0, 8], [1, 16]], eq, -BIG, 0, -1)]
-    g.wait_ge(S.cst, ncst)
-    for k, make in enumerate(made):
-        if k:
-            g.wait_ge(S.gcs, k)
-        make().then_inc(S.gcs, 1)
-    ngcs = len(made)
+    v.tensor_copy(out=T.one[:], in_=T.onb[:]).then_inc(S.chf, 1)
+    v.tensor_copy(out=T.ly[:], in_=T.lyb[:]).then_inc(S.chf, 1)
+    v.tensor_copy(out=T.lx[:], in_=T.lxb[:]).then_inc(S.chf, 1)
+    v.memset(T.rs[:, 0:128:16], -2 * BIG).then_inc(S.chf, 1)
 
-    v.wait_ge(S.cst, ncst)
-    v.wait_ge(S.gcs, ngcs)
-    pe.wait_ge(S.cst, ncst)
-    pe.wait_ge(S.gcs, ngcs)
-    ns = len(_bits(_common([(cores[0], core)], topo)))
+    v.wait_ge(S.cc3, 2)
+    v.wait_ge(S.chf, 4)
+    v.wait_ge(S.csel, 2)
+    pe.wait_ge(S.chf, 4)
+    ns = len(_bits(_common([(cores[LISTER], w) for w in _workers(cores, topo)], topo)))
     v.wait_ge(S.stin, ns)
-    v.tensor_scalar(out=T.ci[:, 0:4], in0=T.s4[:], scalar1=7, scalar2=None,
-                    op0=AluOpType.logical_shift_right).then_inc(S.ini, 1)
-    v.tensor_scalar(out=T.ci[:, 4:8], in0=T.s4[:], scalar1=127, scalar2=None,
-                    op0=AluOpType.bitwise_and).then_inc(S.ini, 1)
+    v.tensor_scalar(out=T.ci[:, 0:4], in0=T.s4[:], scalar1=MX, scalar2=None, op0=band).then_inc(S.ini, 1)
+    v.tensor_scalar(out=T.ci[:, 4:8], in0=T.s4[:], scalar1=MY, scalar2=None, op0=band).then_inc(S.ini, 1)
     v.wait_ge(S.ini, 2)
-    v.tensor_copy(out=T.cf[:], in_=T.ci[:]).then_inc(S.ini, 1)
+    v.tensor_scalar(out=T.cf[:], in0=T.ci[:], scalar1=-float(SH), scalar2=None, op0=add).then_inc(S.ini, 1)
     v.wait_ge(S.ini, 3)
-    for k in range(2):
+    for k, q in ((1, "Y"), (0, "X")):
         for l in range(4):
             v.tensor_scalar(out=T.rr[:, 2 * k:2 * k + 2, 16 * l:16 * l + 16], in0=T.sel[:],
-                            scalar1=T.cf[:, 4 * k + l:4 * k + l + 1], scalar2=None, op0=mult).then_inc(S.ini, 1)
-    pe.wait_ge(S.ini, 11)
+                            scalar1=T.cf[:, 4 * k + l:4 * k + l + 1], scalar2=None, op0=mult).then_inc(S["ini" + q], 1)
+    pe.wait_ge(S.iniY, 4)
     for a, h in enumerate(H):
         pe.matmul(T["py" + h][:, 0:64], T.one[:], T.rr[:, 2 + a, :], True, True).then_inc(S["pY" + h], 1)
+    pe.wait_ge(S.iniX, 4)
+    for a, h in enumerate(H):
         pe.matmul(T["px" + h][:, 0:64], T.one[:], T.rr[:, a, :], True, True).then_inc(S["pX" + h], 1)
 
     def onehots(h, n):
@@ -252,6 +304,8 @@ def _worker(g, core, r, cores, T, topo):
                 for k in range(2):
                     if nscan[k]:
                         v.wait_ge(S["vS%d" % k], nscan[k])
+                if t == NT:
+                    v.wait_ge(S.vL, 2)
                 t0 = steps[0] - 1
                 v.tensor_copy(out=T.offo[:, CB * t0:CB * t],
                               in_=T.sc[:, 128 * t0 + 15:128 * t:16]).then_inc(S["cp%d" % b], 1)
@@ -261,35 +315,38 @@ def _worker(g, core, r, cores, T, topo):
         before = len([u for u in range(1, t) if u % 2 == k])
         if before:
             pe.wait_ge(S["vS%d" % k], before)
+        else:
+            pe.wait_ge(S.cbase, 2)
         pe.matmul(T["po%d" % k][:, 0:128], T.e16[:], T.bt[:], True, False)
 
     def states(t):
-        pe.matmul(T["po%d" % (t % 2)][:, 0:128], T.lf[:], T["z%d" % (t % 2)][:], False, True).then_inc(S.pO, 1)
+        pe.matmul(T["po%d" % (t % 2)][:, 0:128], T.one[:], T["z%d" % (t % 2)][:], False, True).then_inc(S.pO, 1)
 
     for h in H:
         onehots(h, 1)
-    for t in range(1, N):
+    for t in range(1, NT + 1):
         f = N - t
         z = T["z%d" % (t % 2)]
-        pe.wait_ge(S["m%d" % f], len(_bits(_common([(cores[f], core)], topo))))
+        pe.wait_ge(S["m%d" % f], len(_bits(_common([(cores[f], w) for w in _workers(cores, topo)], topo))))
         for h in H:
             pe.wait_ge(S["vY" + h], t)
             pe.matmul(T["pt" + h][:, 0:64], T.tbl[:, 128 * f:128 * f + 128], T["oh" + h][:], True,
                       True).then_inc(S["pT" + h], 1)
         if t > 1:
             states(t - 1)
-        if t == LAST:
-            base(t)
+        if t == NT:
+            for h in H:
+                pe.matmul(T["py" + h][:, 0:64], T.e16[:], T.bt[:, 0:64], True, False)
         for a, h in enumerate(H):
             pe.wait_ge(S["vZ" + h], t)
-            if t < LAST:
-                zh = z[:, 64 * a:64 * a + 64]
+            zh = z[:, 64 * a:64 * a + 64]
+            if t < NT:
                 pe.matmul(T["py" + h][:, 0:64], T.ly[:], zh, True, True).then_inc(S["pY" + h], 1)
                 pe.matmul(T["px" + h][:, 0:64], T.lx[:], zh, True, True).then_inc(S["pX" + h], 1)
-        if t < LAST:
+            else:
+                pe.matmul(T["py" + h][:, 0:64], T.one[:], zh, False, True).then_inc(S["pY" + h], 1)
+        if t < NT:
             base(t)
-        else:
-            states(t)
         for a, h in enumerate(H):
             v.wait_ge(S["vX" + h], t)
             v.wait_ge(S["pT" + h], t)
@@ -297,22 +354,27 @@ def _worker(g, core, r, cores, T, topo):
                             op=mult).then_inc(S["vZ" + h], 1)
         if t > 1:
             scan(t - 1)
-        if t < LAST:
+        if t < NT:
             onehots("A", t + 1)
             pack(t - 1)
             onehots("B", t + 1)
         else:
             pack(t - 1)
-            scan(t)
+            for a, h in enumerate(H):
+                v.wait_ge(S["pY" + h], NT + 1)
+                c = 128 * (NT - 1) + 64 * a
+                v.tensor_tensor_scan(T.sc[:, c:c + 64], T.rs[:, 0:64], T["py" + h][:, 0:64], 0.0,
+                                     add, AluOpType.max).then_inc(S.vL, 1)
             pack(t)
 
     total = 0
     for b, steps in enumerate(BATCHES):
-        m = _common([(core, cores[LAST - t]) for t in steps], topo)
+        masks = _batch_masks(b, core, cores, topo)
         g.wait_ge(S["cp%d" % b], 1)
-        g.remote_dma_fused([RemoteDMATransfer(dst_ids=[_dst(cores[LAST - t], core, topo)], dma_engine_mask=mm,
-                                              remote_sem=S.offin, srcs=[T.offo[:, CB * (t - 1):CB * t]],
-                                              dsts=[T.off[:, CB * r:CB * r + CB]])
-                            for t, mm in zip(steps, _split(m, len(steps)))], local_sem=S.gone)
-        total += len(_bits(m))
+        g.remote_dma_fused([RemoteDMATransfer(dst_ids=[_dst(cores[f], core, topo) for f in _takers(t)],
+                                              dma_engine_mask=mm, remote_sem=S.offin,
+                                              srcs=[T.offo[:, CB * (t - 1):CB * t]],
+                                              dsts=[T.off[:, CB * r:CB * r + CB] for f in _takers(t)])
+                            for t, mm in zip(steps, masks)], local_sem=S.gone)
+        total += sum(len(_bits(mm)) for mm in masks)
     g.wait_ge(S.gone, total)

@@ -6,12 +6,19 @@ NW = 4
 EB = 128
 CB = EB // 16
 LAST = N - 1
-NT = N - 2
-LISTER = 2
-BATCHES = [[1, 2, 3, 4], [5, 6], [7, 8], [9], [10]]
-FIRST = {11: 0, 10: 512, 9: 1024, 8: 1024, 7: 1536, 6: 1536, 5: 2048, 4: 2048, 3: 2048, 2: 2048, 1: 0, 0: 8192}
+PAIRS = [3]
+SEQ = [f for f in range(LAST, 1, -1) if f + 1 not in PAIRS]
+RES = [f - 2 if f in PAIRS else f - 1 for f in SEQ]
+NT = len(SEQ)
+WHOLE = {0: 1}
+for _f in PAIRS:
+    WHOLE[_f - 1] = _f
+LISTERS = [11, 1, 4, 5]
+BATCHES = [[1, 2, 3, 4], [5, 6], [7], [8], [9]]
+FIRST = {11: 0, 10: 512, 9: 1024, 8: 1024, 7: 1536, 6: 1536, 5: 2048, 4: 2048, 3: 0, 2: 1024, 1: 0, 0: 8192}
 BIG = 16384.0
-MX, MY = 0x11F0, 0x0E0F
+STD = (0x11F0, 0x0E0F)
+TWO = (0x118E, 0x0E71)
 SH = 2048
 
 SCRATCH = {
@@ -21,16 +28,28 @@ SCRATCH = {
     "of1": ("sbuf", [128, 512], "uint16"),
     "two": ("sbuf", [128, 128], "int32"),
     "tb": ("sbuf", [128, 128], "float16"),
+    "hls": ("sbuf", [128, 128], "uint16"),
     "st8": ("sbuf", [128, 32], "int32"),
     "off": ("sbuf", [128, 32], "uint16"),
     "win": ("sbuf", [128, 8192], "float32"),
     "win1": ("sbuf", [128, 8192], "float32"),
     "yy": ("sbuf", [128, 512], "float32"),
     "s4": ("sbuf", [128, 4], "int32"),
+    "dw": ("dram", [128, 64], "int32"),
+    "hl": ("sbuf", [128, 64], "uint16"),
+    "winf": ("sbuf", [128, 512], "float32"),
+    "row": ("sbuf", [128, 16], "int32"),
+    "rowf": ("sbuf", [128, 16], "float32"),
+    "w2": ("sbuf", [128, 16], "bfloat16"),
+    "gs": ("sbuf", [128, 8], "float32"),
+    "ox": ("sbuf", [128, 512], "bfloat16"),
+    "zc": ("sbuf", [128, 512], "float32"),
+    "cci": ("sbuf", [128, 32], "int32"),
     "tbl": ("sbuf", [128, N * 128], "float16"),
     "ip": ("sbuf", [128, 1], "int32"),
-    "ic": ("sbuf", [128, 4], "int32"),
-    "fc": ("sbuf", [128, 4], "float32"),
+    "ic": ("sbuf", [128, 8], "int32"),
+    "fc": ("sbuf", [128, 9], "float32"),
+    "fd": ("sbuf", [128, 2], "float32"),
     "ci": ("sbuf", [128, 8], "int32"),
     "cf": ("sbuf", [128, 8], "float32"),
     "rr": ("sbuf", [128, 4, 64], "float16"),
@@ -47,6 +66,8 @@ SCRATCH = {
     "rs": ("sbuf", [128, 128], "float32"),
     "yc": ("sbuf", [128, 1], "float32"),
     "xc": ("sbuf", [128, 1], "float32"),
+    "yc2": ("sbuf", [128, 1], "float32"),
+    "xc2": ("sbuf", [128, 1], "float32"),
     "ohA": ("sbuf", [128, 64], "float16"),
     "ohB": ("sbuf", [128, 64], "float16"),
     "mxA": ("sbuf", [128, 64], "float16"),
@@ -64,11 +85,12 @@ SCRATCH = {
     "po0": ("psum", [128, 512], "float32"),
     "po1": ("psum", [128, 512], "float32"),
 }
-SEMAPHORES = (["ld", "ls", "prep", "left", "leftl", "offin", "tab0", "tabin", "stin", "st8in", "offok", "comp", "yv", "ya",
-               "ys", "cbf", "cst", "chf", "cip", "csel", "cbase", "cc1", "cc2", "cc3", "ini", "iniY", "iniX", "pO", "vS0",
+SEMAPHORES = (["ld", "ld8", "ls", "prep", "prep8", "left", "left8", "leftl", "offin", "tab0", "tabin", "stin", "st8in", "offok",
+               "comp", "yv", "ya", "ys", "of1in", "dwin", "hlin", "wl", "k1", "k2", "k3", "kw", "oxs", "zs", "cs", "cbf",
+               "cst", "chf", "cip", "csel", "cbase", "cc1", "cc2", "cc3", "cc4", "ini", "iniY", "iniX", "pO", "vS0",
                "vS1", "vL", "gone"]
               + [k + h for k in ("pT", "pY", "pX", "vZ", "vY", "vX") for h in "AB"]
-              + ["m%d" % f for f in range(1, N)] + ["cp%d" % b for b in range(len(BATCHES))])
+              + ["m%d" % f for f in SEQ] + ["cp%d" % b for b in range(len(BATCHES))])
 
 
 def _bits(mask):
@@ -81,21 +103,31 @@ def _split(mask, n):
     return [sum(e[k * i:k * i + k]) for i in range(n)]
 
 
+def _at(c, topo):
+    return (topo.host(c), topo.chip(c))
+
+
 def _workers(cores, topo):
-    def at(c):
-        return (topo.host(c), topo.chip(c))
-    used = {at(c) for c in cores}
+    used = {_at(c, topo) for c in cores}
     got = {True: [], False: []}
     for c in range(256):
-        if at(c) in used or topo.die(c) != topo.die(cores[0]):
+        if _at(c, topo) in used or topo.die(c) != topo.die(cores[0]):
             continue
         if not all(topo.may_write(c, d) and topo.may_write(d, c) for d in cores):
             continue
         k = topo.same_plane(c, cores[0])
         if len(got[k]) < NW // 2:
             got[k].append(c)
-            used.add(at(c))
+            used.add(_at(c, topo))
     return got[True] + got[False]
+
+
+def _helpers(f, cores, workers, topo):
+    own = cores[f - 1]
+    got = [c for c in range(256) if c != own and _at(c, topo) == _at(own, topo)
+           and all(topo.may_write(c, w) for w in workers) and topo.may_write(cores[f], c)]
+    got.sort(key=lambda c: topo.die(c) != topo.die(own))
+    return got[:2]
 
 
 def _common(srcs_dsts, topo):
@@ -105,18 +137,34 @@ def _common(srcs_dsts, topo):
     return m
 
 
+def _count(src, dsts, topo):
+    return len(_bits(_common([(src, d) for d in dsts], topo)))
+
+
 def _dst(d, core, topo):
     rid, pid = topo.addr(d, core)
     return DstId(rid=rid, pnc=pid)
 
 
 def _takers(t):
-    return [LAST - t] if t < NT else [LAST - t, 0]
+    b = RES[t - 1]
+    return [b] + [r for r in sorted(WHOLE) if WHOLE[r] == b]
+
+
+def _codes(k):
+    return TWO if k + 1 < NT and SEQ[k + 1] in PAIRS else STD
 
 
 def _batch_masks(b, w, cores, topo):
     m = _common([(w, cores[f]) for t in BATCHES[b] for f in _takers(t)], topo)
     return _split(m, len(BATCHES[b]))
+
+
+def _send(g, core, src, dst, to, sem, left, topo):
+    mask = _common([(core, c) for c in to], topo)
+    g.remote_dma_fused([RemoteDMATransfer(dst_ids=[_dst(c, core, topo) for c in to], dma_engine_mask=mask,
+                                          remote_sem=sem, srcs=[src], dsts=[dst for c in to])], local_sem=left)
+    return len(_bits(mask))
 
 
 def rank_program(g, core, T, topo):
@@ -126,56 +174,86 @@ def rank_program(g, core, T, topo):
     if rank is not None:
         _rank(g, core, rank, cores, workers, T, topo)
     elif core in workers:
-        _worker(g, core, workers.index(core), cores, T, topo)
+        _worker(g, core, workers.index(core), cores, workers, T, topo)
+    else:
+        for f in PAIRS:
+            hs = _helpers(f, cores, workers, topo)
+            if core in hs:
+                _helper(g, core, f, hs.index(core), cores, workers, T, topo)
+
+
+def _encode(v, src, n, masks, T, sem):
+    for k in range(2):
+        v.tensor_scalar(out=T.two[:, n * k:n * k + n], in0=src, scalar1=masks[k], scalar2=None,
+                        op0=AluOpType.bitwise_and).then_inc(sem, 1)
+    v.wait_ge(sem, 2)
+    v.tensor_scalar(out=T.tb[:, 0:2 * n], in0=T.two[:, 0:2 * n], scalar1=-float(SH), scalar2=None,
+                    op0=AluOpType.add).then_inc(sem, 1)
 
 
 def _rank(g, core, f, cores, workers, T, topo):
     v, act, sync, S = g.vector, g.scalar, g.sync, T.sem
     first = FIRST[f]
+    source = f in WHOLE.values()
+    taken = f + 1 in PAIRS
+    lister = f in LISTERS
 
-    def send(src, dst, to, sem, left):
-        mask = _common([(core, c) for c in to], topo)
-        g.remote_dma_fused([RemoteDMATransfer(dst_ids=[_dst(c, core, topo) for c in to], dma_engine_mask=mask,
-                                              remote_sem=sem, srcs=[src], dsts=[dst for c in to])], local_sem=left)
-        return len(_bits(mask))
-
-    if f == LISTER:
+    if lister:
         sync.dma_start(out=T.s4[:], in_=T.st[:]).then_inc(S.ls, 16)
-    if f > 1:
+    if taken:
+        sync.dma_start(out=T.raw[:], in_=T.bp[:]).then_inc(S.ld, 16)
+    elif f > 1:
         for a, q in enumerate((sync, act)):
             q.dma_start(out=T.raw[:, 32 * a:32 * a + 32], in_=T.bp[:, 256 * a:256 * a + 256]).then_inc(S.ld, 16)
-    elif f == 1:
+    if source:
         for b in range(8):
             q = sync if b % 2 == 0 else act
-            q.dma_start(out=T.raw8[16 * b:16 * b + 16, :], in_=T.bp[:]).then_inc(S.ld, 16)
-    if f == LISTER:
+            q.dma_start(out=T.raw8[16 * b:16 * b + 16, :], in_=T.bp[:]).then_inc(S.ld8, 16)
+    if lister:
         g.wait_ge(S.ls, 16)
-        nl = send(T.s4[:], T.s4[:], workers, S.stin, S.leftl)
+        nl = _send(g, core, T.s4[:], T.s4[:], [workers[LISTERS.index(f)]], S.stin, S.leftl, topo)
         sync.wait_ge(S.leftl, nl)
     if first:
         sync.dma_start(out=T.win[:, 0:first], in_=T.tab[:, 0:first]).then_inc(S.tab0, 16)
 
-    if f > 1:
+    ne = 0
+    if taken:
+        g.wait_ge(S.ld, 16)
+        ne = _send(g, core, T.raw[:], T.dw[:], _helpers(f + 1, cores, workers, topo), S.dwin, S.left, topo)
+    elif f in PAIRS:
         v.wait_ge(S.ld, 32)
-        v.tensor_scalar(out=T.two[:, 0:64], in0=T.raw[:], scalar1=MX, scalar2=None,
-                        op0=AluOpType.bitwise_and).then_inc(S.prep, 1)
-        v.tensor_scalar(out=T.two[:, 64:128], in0=T.raw[:], scalar1=MY, scalar2=None,
-                        op0=AluOpType.bitwise_and).then_inc(S.prep, 1)
-        v.wait_ge(S.prep, 2)
-        v.tensor_scalar(out=T.tb[:], in0=T.two[:], scalar1=-float(SH), scalar2=None,
-                        op0=AluOpType.add).then_inc(S.prep, 1)
+        for a in range(2):
+            for k, (op, c) in enumerate(((AluOpType.logical_shift_right, 4), (AluOpType.bitwise_and, 15))):
+                v.tensor_scalar(out=T.two[:, 64 * a + 32 * k:64 * a + 32 * k + 32], in0=T.raw[:, 32 * a:32 * a + 32],
+                                scalar1=c, scalar2=None, op0=op).then_inc(S.prep, 1)
+        v.wait_ge(S.prep, 4)
+        v.tensor_copy(out=T.hls[:], in_=T.two[:]).then_inc(S.prep, 1)
+        hs = _helpers(f, cores, workers, topo)
+        m = _common([(core, h) for h in hs], topo)
+        g.wait_ge(S.prep, 5)
+        g.remote_dma_fused([RemoteDMATransfer(dst_ids=[_dst(h, core, topo)], dma_engine_mask=mm, remote_sem=S.hlin,
+                                              srcs=[T.hls[:, 64 * a:64 * a + 64]], dsts=[T.hl[:]])
+                            for a, (h, mm) in enumerate(zip(hs, _split(m, 2)))], local_sem=S.left)
+        ne = len(_bits(m))
+    elif f > 1:
+        v.wait_ge(S.ld, 32)
+        _encode(v, T.raw[:], 64, _codes(SEQ.index(f)), T, S.prep)
         g.wait_ge(S.prep, 3)
         if first:
             g.wait_ge(S.tab0, 16)
-        ne = send(T.tb[:], T.tbl[:, 128 * f:128 * f + 128], workers, S["m%d" % f], S.left)
-    elif f == 1:
-        v.wait_ge(S.ld, 128)
-        v.tensor_copy(out=T.of1s[:], in_=T.raw8[:]).then_inc(S.prep, 1)
-        g.wait_ge(S.prep, 1)
-        ne = send(T.of1s[:], T.of1[:], [cores[0]], S.m1, S.left)
+        ne = _send(g, core, T.tb[:], T.tbl[:, 128 * f:128 * f + 128], workers, S["m%d" % f], S.left, topo)
+    n8 = 0
+    if source:
+        v.wait_ge(S.ld8, 128)
+        v.tensor_copy(out=T.of1s[:], in_=T.raw8[:]).then_inc(S.prep8, 1)
+        g.wait_ge(S.prep8, 1)
+        n8 = _send(g, core, T.of1s[:], T.of1[:], [cores[f - 1]], S.of1in, S.left8, topo)
 
     if first < 8192:
-        sync.wait_ge(S.left, ne)
+        if ne:
+            sync.wait_ge(S.left, ne)
+        if n8:
+            sync.wait_ge(S.left8, n8)
         sync.dma_start(out=T.win[:, first:8192], in_=T.tab[:, first:8192]).then_inc(S.tabin, 16)
 
     def tab_there(q):
@@ -201,12 +279,12 @@ def _rank(g, core, f, cores, workers, T, topo):
     win = T.win
     tab_there(v)
     tab_there(act)
-    if f == 0:
-        n1 = len(_bits(_common([(cores[1], core)], topo)))
+    if f in WHOLE:
+        n1 = _count(cores[f + 1], [core], topo)
         win = T.win1
-        v.wait_ge(S.m1, n1)
+        v.wait_ge(S.of1in, n1)
         v.tensor_copy(out=win[:, 0:4096], in_=T.win[:].indirect(T.of1[:, 0:256])).then_inc(S.comp, 1)
-        act.wait_ge(S.m1, n1)
+        act.wait_ge(S.of1in, n1)
         act.activation(out=win[:, 4096:8192], in_=T.win[:].indirect(T.of1[:, 256:512]),
                        func=ActivationFunctionType.Copy, bias=-0.0).then_inc(S.comp, 1)
         v.wait_ge(S.comp, 2)
@@ -223,7 +301,56 @@ def _rank(g, core, f, cores, workers, T, topo):
     sync.wait_ge(S.ys, 32)
 
 
-def _worker(g, core, r, cores, T, topo):
+def _helper(g, core, f, m, cores, workers, T, topo):
+    v, act, pe, sync, S = g.vector, g.scalar, g.tensor, g.sync, T.sem
+    eq, mult = AluOpType.is_equal, AluOpType.mult
+    g.iota(T.ip[:], [[0, 1]], 0, 1).then_inc(S.cip, 1)
+    g.iota(T.row[:], [[1, 16]], 0, 0).then_inc(S.cip, 1)
+    v.wait_ge(S.cip, 2)
+    v.tensor_scalar(out=T.ic[:, 0:1], in0=T.ip[:], scalar1=15, scalar2=None, op0=AluOpType.bitwise_and).then_inc(S.k1, 1)
+    v.tensor_scalar(out=T.ic[:, 1:2], in0=T.ip[:], scalar1=4, scalar2=None,
+                    op0=AluOpType.logical_shift_right).then_inc(S.k1, 1)
+    v.tensor_copy(out=T.rowf[:], in_=T.row[:]).then_inc(S.k1, 1)
+    v.wait_ge(S.k1, 3)
+    v.tensor_copy(out=T.fc[:, 0:2], in_=T.ic[:, 0:2]).then_inc(S.k2, 1)
+    v.wait_ge(S.k2, 1)
+    v.tensor_scalar(out=T.w2[:], in0=T.rowf[:], scalar1=T.fc[:, 0:1], scalar2=None, op0=eq).then_inc(S.k3, 1)
+    v.tensor_scalar(out=T.gs[:], in0=T.rowf[:, 0:8], scalar1=T.fc[:, 1:2], scalar2=None, op0=eq).then_inc(S.k3, 1)
+
+    nd = _count(cores[f - 1], _helpers(f, cores, workers, topo), topo)
+    for b in range(8):
+        q = sync if b % 2 == 0 else act
+        q.wait_ge(S.dwin, nd)
+        q.dma_start(out=T.raw8[16 * b:16 * b + 16, :], in_=T.dw[:]).then_inc(S.wl, 16)
+    v.wait_ge(S.wl, 128)
+    v.tensor_copy(out=T.winf[:], in_=T.raw8[:]).then_inc(S.kw, 1)
+
+    nh = _count(cores[f], _helpers(f, cores, workers, topo), topo) // 2
+    act.wait_ge(S.k3, 2)
+    act.wait_ge(S.hlin, nh)
+    v.wait_ge(S.hlin, nh)
+    v.wait_ge(S.kw, 1)
+    for k in range(2):
+        act.activation(out=T.ox[:, 256 * k:256 * k + 256], in_=T.w2[:].indirect(T.hl[:, 32 + 16 * k:48 + 16 * k]),
+                       func=ActivationFunctionType.Copy).then_inc(S.oxs, 1)
+        v.wait_ge(S.oxs, k + 1)
+        v.tensor_tensor(out=T.zc[:, 256 * k:256 * k + 256], in0=T.winf[:].indirect(T.hl[:, 16 * k:16 * k + 16]),
+                        in1=T.ox[:, 256 * k:256 * k + 256], op=mult).then_inc(S.zs, 1)
+        if k == 0:
+            pe.wait_ge(S.k3, 2)
+        pe.wait_ge(S.zs, k + 1)
+        for c in (2 * k, 2 * k + 1):
+            pe.matmul(T.ptA[:, 8 * c:8 * c + 8], T.zc[:, 128 * c:128 * c + 128], T.gs[:], True, True).then_inc(S.cs, 1)
+    v.wait_ge(S.cs, 4)
+    v.tensor_copy(out=T.cci[:], in_=T.ptA[:, 0:32]).then_inc(S.k2, 1)
+    v.wait_ge(S.k2, 2)
+    _encode(v, T.cci[:], 32, _codes(SEQ.index(f)), T, S.prep)
+    g.wait_ge(S.prep, 3)
+    ne = _send(g, core, T.tb[:, 0:64], T.tbl[:, 128 * f + 64 * m:128 * f + 64 * m + 64], workers, S["m%d" % f], S.left, topo)
+    g.wait_ge(S.left, ne)
+
+
+def _worker(g, core, r, cores, workers, T, topo):
     v, pe, S = g.vector, g.tensor, T.sem
     H = "AB"
     eq, mult, add = AluOpType.is_equal, AluOpType.mult, AluOpType.add
@@ -244,30 +371,39 @@ def _worker(g, core, r, cores, T, topo):
     for ap, c in fills:
         v.memset(ap, c).then_inc(S.cst, 1)
     v.wait_ge(S.cip, 1)
-    for k, (op, c) in enumerate(((shr, 3), (band, 7), (band, 31), (band, 32))):
-        v.tensor_scalar(out=T.ic[:, k:k + 1], in0=T.ip[:], scalar1=c, scalar2=None, op0=op).then_inc(S.cc1, 1)
-    v.wait_ge(S.cc1, 4)
-    for k, (m, a) in enumerate(((1.0, 0.0), (512.0, -float(SH)), (16.0, -float(SH)), (128.0, 0.0))):
-        v.tensor_scalar(out=T.fc[:, k:k + 1], in0=T.ic[:, k:k + 1], scalar1=m, scalar2=a, op0=mult,
+    bits = ((shr, 3), (band, 7), (band, 31), (band, 32), (band, 112), None, (band, 24), (shr, 6))
+    for k, oc in enumerate(bits):
+        if oc is None:
+            v.tensor_scalar(out=T.ic[:, k:k + 1], in0=T.ip[:], scalar1=3, scalar2=1, op0=shr, op1=band).then_inc(S.cc1, 1)
+        else:
+            v.tensor_scalar(out=T.ic[:, k:k + 1], in0=T.ip[:], scalar1=oc[1], scalar2=None, op0=oc[0]).then_inc(S.cc1, 1)
+    v.wait_ge(S.cc1, 8)
+    sh = -float(SH)
+    lin = ((0, 1.0, 0.0), (1, 512.0, sh), (2, 16.0, sh), (3, 128.0, 0.0), (4, 1.0, 0.0), (5, 1.0, 0.0), (6, 16.0, 0.0),
+           (7, 4096.0, 0.0), (1, 2.0, sh))
+    for k, (j, m, a) in enumerate(lin):
+        v.tensor_scalar(out=T.fc[:, k:k + 1], in0=T.ic[:, j:j + 1], scalar1=m, scalar2=a, op0=mult,
                         op1=add).then_inc(S.cc2, 1)
-    v.wait_ge(S.cc2, 4)
-    v.tensor_tensor(out=T.yc[:], in0=T.fc[:, 0:1], in1=T.fc[:, 1:2], op=add).then_inc(S.cc3, 1)
-    v.tensor_tensor(out=T.xc[:], in0=T.fc[:, 2:3], in1=T.fc[:, 3:4], op=add).then_inc(S.cc3, 1)
+    v.wait_ge(S.cc2, 9)
+    for o, p, q in ((T.yc[:], 0, 1), (T.xc[:], 2, 3), (T.fd[:, 0:1], 4, 5), (T.fd[:, 1:2], 6, 7)):
+        v.tensor_tensor(out=o, in0=T.fc[:, p:p + 1], in1=T.fc[:, q:q + 1], op=add).then_inc(S.cc3, 1)
     v.wait_ge(S.cbf, 2)
     v.wait_ge(S.cst, len(fills))
     v.tensor_copy(out=T.one[:], in_=T.onb[:]).then_inc(S.chf, 1)
     v.tensor_copy(out=T.ly[:], in_=T.lyb[:]).then_inc(S.chf, 1)
     v.tensor_copy(out=T.lx[:], in_=T.lxb[:]).then_inc(S.chf, 1)
     v.memset(T.rs[:, 0:128:16], -2 * BIG).then_inc(S.chf, 1)
+    v.wait_ge(S.cc3, 4)
+    v.tensor_tensor(out=T.yc2[:], in0=T.fd[:, 0:1], in1=T.fc[:, 1:2], op=add).then_inc(S.cc4, 1)
+    v.tensor_tensor(out=T.xc2[:], in0=T.fd[:, 1:2], in1=T.fc[:, 8:9], op=add).then_inc(S.cc4, 1)
 
-    v.wait_ge(S.cc3, 2)
+    v.wait_ge(S.cc4, 2)
     v.wait_ge(S.chf, 4)
     v.wait_ge(S.csel, 2)
     pe.wait_ge(S.chf, 4)
-    ns = len(_bits(_common([(cores[LISTER], w) for w in _workers(cores, topo)], topo)))
-    v.wait_ge(S.stin, ns)
-    v.tensor_scalar(out=T.ci[:, 0:4], in0=T.s4[:], scalar1=MX, scalar2=None, op0=band).then_inc(S.ini, 1)
-    v.tensor_scalar(out=T.ci[:, 4:8], in0=T.s4[:], scalar1=MY, scalar2=None, op0=band).then_inc(S.ini, 1)
+    v.wait_ge(S.stin, _count(cores[LISTERS[r]], [core], topo))
+    v.tensor_scalar(out=T.ci[:, 0:4], in0=T.s4[:], scalar1=STD[0], scalar2=None, op0=band).then_inc(S.ini, 1)
+    v.tensor_scalar(out=T.ci[:, 4:8], in0=T.s4[:], scalar1=STD[1], scalar2=None, op0=band).then_inc(S.ini, 1)
     v.wait_ge(S.ini, 2)
     v.tensor_scalar(out=T.cf[:], in0=T.ci[:], scalar1=-float(SH), scalar2=None, op0=add).then_inc(S.ini, 1)
     v.wait_ge(S.ini, 3)
@@ -283,11 +419,12 @@ def _worker(g, core, r, cores, T, topo):
         pe.matmul(T["px" + h][:, 0:64], T.one[:], T.rr[:, a, :], True, True).then_inc(S["pX" + h], 1)
 
     def onehots(h, n):
+        yc, xc = (T.yc2, T.xc2) if SEQ[n - 1] in PAIRS else (T.yc, T.xc)
         v.wait_ge(S["pY" + h], n)
-        v.tensor_scalar(out=T["oh" + h][:], in0=T["py" + h][:, 0:64], scalar1=T.yc[:, 0:1], scalar2=None,
+        v.tensor_scalar(out=T["oh" + h][:], in0=T["py" + h][:, 0:64], scalar1=yc[:, 0:1], scalar2=None,
                         op0=eq).then_inc(S["vY" + h], 1)
         v.wait_ge(S["pX" + h], n)
-        v.tensor_scalar(out=T["mx" + h][:], in0=T["px" + h][:, 0:64], scalar1=T.xc[:, 0:1], scalar2=None,
+        v.tensor_scalar(out=T["mx" + h][:], in0=T["px" + h][:, 0:64], scalar1=xc[:, 0:1], scalar2=None,
                         op0=eq).then_inc(S["vX" + h], 1)
 
     nscan = [0, 0]
@@ -325,9 +462,10 @@ def _worker(g, core, r, cores, T, topo):
     for h in H:
         onehots(h, 1)
     for t in range(1, NT + 1):
-        f = N - t
+        f = SEQ[t - 1]
         z = T["z%d" % (t % 2)]
-        pe.wait_ge(S["m%d" % f], len(_bits(_common([(cores[f], w) for w in _workers(cores, topo)], topo))))
+        senders = _helpers(f, cores, workers, topo) if f in PAIRS else [cores[f]]
+        pe.wait_ge(S["m%d" % f], sum(_count(s, workers, topo) for s in senders))
         for h in H:
             pe.wait_ge(S["vY" + h], t)
             pe.matmul(T["pt" + h][:, 0:64], T.tbl[:, 128 * f:128 * f + 128], T["oh" + h][:], True,

@@ -6,16 +6,17 @@ NW = 4
 EB = 128
 CB = EB // 16
 LAST = N - 1
-PAIRS = [3]
+PAIRS = [5, 3]
 SEQ = [f for f in range(LAST, 1, -1) if f + 1 not in PAIRS]
 RES = [f - 2 if f in PAIRS else f - 1 for f in SEQ]
 NT = len(SEQ)
 WHOLE = {0: 1}
 for _f in PAIRS:
     WHOLE[_f - 1] = _f
-LISTERS = [11, 1, 4, 5]
-BATCHES = [[1, 2, 3, 4], [5, 6], [7], [8], [9]]
-FIRST = {11: 0, 10: 512, 9: 1024, 8: 1024, 7: 1536, 6: 1536, 5: 2048, 4: 2048, 3: 0, 2: 1024, 1: 0, 0: 8192}
+LISTERS = [11, 1, 6, 7]
+BATCHES = [[1, 2, 3, 4], [5], [6], [7], [8]]
+FIRST = {11: 0, 10: 512, 9: 1024, 8: 1024, 7: 1536, 6: 1536, 5: 0, 4: 1536, 3: 0, 2: 2048, 1: 0, 0: 8192}
+NEXT = 1024
 BIG = 16384.0
 STD = (0x11F0, 0x0E0F)
 TWO = (0x118E, 0x0E71)
@@ -24,6 +25,7 @@ SH = 2048
 SCRATCH = {
     "raw": ("sbuf", [128, 64], "int32"),
     "raw8": ("sbuf", [128, 512], "int32"),
+    "dws": ("dram", [128, 64], "int32"),
     "of1s": ("sbuf", [128, 512], "uint16"),
     "of1": ("sbuf", [128, 512], "uint16"),
     "two": ("sbuf", [128, 128], "int32"),
@@ -37,7 +39,6 @@ SCRATCH = {
     "s4": ("sbuf", [128, 4], "int32"),
     "dw": ("dram", [128, 64], "int32"),
     "hl": ("sbuf", [128, 64], "uint16"),
-    "winf": ("sbuf", [128, 512], "float32"),
     "row": ("sbuf", [128, 16], "int32"),
     "rowf": ("sbuf", [128, 16], "float32"),
     "w2": ("sbuf", [128, 16], "bfloat16"),
@@ -48,7 +49,7 @@ SCRATCH = {
     "tbl": ("sbuf", [128, N * 128], "float16"),
     "ip": ("sbuf", [128, 1], "int32"),
     "ic": ("sbuf", [128, 8], "int32"),
-    "fc": ("sbuf", [128, 9], "float32"),
+    "fc": ("sbuf", [128, 11], "float32"),
     "fd": ("sbuf", [128, 2], "float32"),
     "ci": ("sbuf", [128, 8], "int32"),
     "cf": ("sbuf", [128, 8], "float32"),
@@ -61,6 +62,8 @@ SCRATCH = {
     "one": ("sbuf", [128, 128], "float16"),
     "ly": ("sbuf", [128, 128], "float16"),
     "lx": ("sbuf", [128, 128], "float16"),
+    "ly2": ("sbuf", [128, 128], "float16"),
+    "lx2": ("sbuf", [128, 128], "float16"),
     "e16": ("sbuf", [16, 128], "bfloat16"),
     "bt": ("sbuf", [16, 128], "bfloat16"),
     "rs": ("sbuf", [128, 128], "float32"),
@@ -85,10 +88,10 @@ SCRATCH = {
     "po0": ("psum", [128, 512], "float32"),
     "po1": ("psum", [128, 512], "float32"),
 }
-SEMAPHORES = (["ld", "ld8", "ls", "prep", "prep8", "left", "left8", "leftl", "offin", "tab0", "tabin", "stin", "st8in", "offok",
-               "comp", "yv", "ya", "ys", "of1in", "dwin", "hlin", "wl", "k1", "k2", "k3", "kw", "oxs", "zs", "cs", "cbf",
-               "cst", "chf", "cip", "csel", "cbase", "cc1", "cc2", "cc3", "cc4", "ini", "iniY", "iniX", "pO", "vS0",
-               "vS1", "vL", "gone"]
+SEMAPHORES = (["ld", "ld8", "ls", "prep", "prep8", "left", "left8", "leftl", "offin", "tab0", "tab1", "tab2", "tabin", "go",
+               "stin", "st8in", "offok", "comp", "yv", "ya", "ys", "of1in", "dwin", "hlin", "wl", "k1", "k2", "k3", "oxs", "zs",
+               "cs", "cbf", "cst", "chf", "cl2", "cip", "csel", "cbase", "cc1", "cc2", "cc3", "cc4", "ini", "iniY", "iniX",
+               "pO", "vS0", "vS1", "vL", "gone"]
               + [k + h for k in ("pT", "pY", "pX", "vZ", "vY", "vX") for h in "AB"]
               + ["m%d" % f for f in SEQ] + ["cp%d" % b for b in range(len(BATCHES))])
 
@@ -201,7 +204,7 @@ def _rank(g, core, f, cores, workers, T, topo):
     if lister:
         sync.dma_start(out=T.s4[:], in_=T.st[:]).then_inc(S.ls, 16)
     if taken:
-        sync.dma_start(out=T.raw[:], in_=T.bp[:]).then_inc(S.ld, 16)
+        sync.dma_start(out=T.dws[:], in_=T.bp[:]).then_inc(S.ld, 16)
     elif f > 1:
         for a, q in enumerate((sync, act)):
             q.dma_start(out=T.raw[:, 32 * a:32 * a + 32], in_=T.bp[:, 256 * a:256 * a + 256]).then_inc(S.ld, 16)
@@ -217,9 +220,15 @@ def _rank(g, core, f, cores, workers, T, topo):
         sync.dma_start(out=T.win[:, 0:first], in_=T.tab[:, 0:first]).then_inc(S.tab0, 16)
 
     ne = 0
+    rest = first
     if taken:
         g.wait_ge(S.ld, 16)
-        ne = _send(g, core, T.raw[:], T.dw[:], _helpers(f + 1, cores, workers, topo), S.dwin, S.left, topo)
+        ne = _send(g, core, T.dws[:], T.dw[:], _helpers(f + 1, cores, workers, topo), S.dwin, S.left, topo)
+        g.sem_inc(S.go, 1)
+        for gate, n, done in ((S.go, 1, S.tab1), (S.tab0, 16, S.tab2)):
+            sync.wait_ge(gate, n)
+            sync.dma_start(out=T.win[:, rest:rest + NEXT], in_=T.tab[:, rest:rest + NEXT]).then_inc(done, 16)
+            rest += NEXT
     elif f in PAIRS:
         v.wait_ge(S.ld, 32)
         for a in range(2):
@@ -249,17 +258,20 @@ def _rank(g, core, f, cores, workers, T, topo):
         g.wait_ge(S.prep8, 1)
         n8 = _send(g, core, T.of1s[:], T.of1[:], [cores[f - 1]], S.of1in, S.left8, topo)
 
-    if first < 8192:
+    if rest < 8192:
         if ne:
             sync.wait_ge(S.left, ne)
         if n8:
             sync.wait_ge(S.left8, n8)
-        sync.dma_start(out=T.win[:, first:8192], in_=T.tab[:, first:8192]).then_inc(S.tabin, 16)
+        sync.dma_start(out=T.win[:, rest:8192], in_=T.tab[:, rest:8192]).then_inc(S.tabin, 16)
 
     def tab_there(q):
         if first:
             q.wait_ge(S.tab0, 16)
-        if first < 8192:
+        if taken:
+            q.wait_ge(S.tab1, 16)
+            q.wait_ge(S.tab2, 16)
+        if rest < 8192:
             q.wait_ge(S.tabin, 16)
 
     if f == LAST:
@@ -322,25 +334,22 @@ def _helper(g, core, f, m, cores, workers, T, topo):
         q = sync if b % 2 == 0 else act
         q.wait_ge(S.dwin, nd)
         q.dma_start(out=T.raw8[16 * b:16 * b + 16, :], in_=T.dw[:]).then_inc(S.wl, 16)
-    v.wait_ge(S.wl, 128)
-    v.tensor_copy(out=T.winf[:], in_=T.raw8[:]).then_inc(S.kw, 1)
 
     nh = _count(cores[f], _helpers(f, cores, workers, topo), topo) // 2
     act.wait_ge(S.k3, 2)
     act.wait_ge(S.hlin, nh)
     v.wait_ge(S.hlin, nh)
-    v.wait_ge(S.kw, 1)
-    for k in range(2):
-        act.activation(out=T.ox[:, 256 * k:256 * k + 256], in_=T.w2[:].indirect(T.hl[:, 32 + 16 * k:48 + 16 * k]),
+    v.wait_ge(S.wl, 128)
+    pe.wait_ge(S.k3, 2)
+    for k in range(4):
+        c = slice(128 * k, 128 * k + 128)
+        act.activation(out=T.ox[:, c], in_=T.w2[:].indirect(T.hl[:, 32 + 8 * k:40 + 8 * k]),
                        func=ActivationFunctionType.Copy).then_inc(S.oxs, 1)
         v.wait_ge(S.oxs, k + 1)
-        v.tensor_tensor(out=T.zc[:, 256 * k:256 * k + 256], in0=T.winf[:].indirect(T.hl[:, 16 * k:16 * k + 16]),
-                        in1=T.ox[:, 256 * k:256 * k + 256], op=mult).then_inc(S.zs, 1)
-        if k == 0:
-            pe.wait_ge(S.k3, 2)
+        v.tensor_tensor(out=T.zc[:, c], in0=T.raw8[:].indirect(T.hl[:, 8 * k:8 * k + 8]), in1=T.ox[:, c],
+                        op=mult).then_inc(S.zs, 1)
         pe.wait_ge(S.zs, k + 1)
-        for c in (2 * k, 2 * k + 1):
-            pe.matmul(T.ptA[:, 8 * c:8 * c + 8], T.zc[:, 128 * c:128 * c + 128], T.gs[:], True, True).then_inc(S.cs, 1)
+        pe.matmul(T.ptA[:, 8 * k:8 * k + 8], T.zc[:, c], T.gs[:], True, True).then_inc(S.cs, 1)
     v.wait_ge(S.cs, 4)
     v.tensor_copy(out=T.cci[:], in_=T.ptA[:, 0:32]).then_inc(S.k2, 1)
     v.wait_ge(S.k2, 2)
@@ -380,11 +389,11 @@ def _worker(g, core, r, cores, workers, T, topo):
     v.wait_ge(S.cc1, 8)
     sh = -float(SH)
     lin = ((0, 1.0, 0.0), (1, 512.0, sh), (2, 16.0, sh), (3, 128.0, 0.0), (4, 1.0, 0.0), (5, 1.0, 0.0), (6, 16.0, 0.0),
-           (7, 4096.0, 0.0), (1, 2.0, sh))
+           (7, 4096.0, 0.0), (1, 2.0, sh), (3, 0.03125, 0.0), (3, -0.03125, 1.0))
     for k, (j, m, a) in enumerate(lin):
         v.tensor_scalar(out=T.fc[:, k:k + 1], in0=T.ic[:, j:j + 1], scalar1=m, scalar2=a, op0=mult,
                         op1=add).then_inc(S.cc2, 1)
-    v.wait_ge(S.cc2, 9)
+    v.wait_ge(S.cc2, len(lin))
     for o, p, q in ((T.yc[:], 0, 1), (T.xc[:], 2, 3), (T.fd[:, 0:1], 4, 5), (T.fd[:, 1:2], 6, 7)):
         v.tensor_tensor(out=o, in0=T.fc[:, p:p + 1], in1=T.fc[:, q:q + 1], op=add).then_inc(S.cc3, 1)
     v.wait_ge(S.cbf, 2)
@@ -461,15 +470,20 @@ def _worker(g, core, r, cores, workers, T, topo):
 
     for h in H:
         onehots(h, 1)
+    v.tensor_scalar(out=T.ly2[:], in0=T.onb[:], scalar1=T.fc[:, 9:10], scalar2=None, op0=mult).then_inc(S.cl2, 1)
+    v.tensor_scalar(out=T.lx2[:], in0=T.onb[:], scalar1=T.fc[:, 10:11], scalar2=None, op0=mult).then_inc(S.cl2, 1)
     for t in range(1, NT + 1):
         f = SEQ[t - 1]
         z = T["z%d" % (t % 2)]
+        ly, lx = (T.ly2, T.lx2) if f in PAIRS else (T.ly, T.lx)
         senders = _helpers(f, cores, workers, topo) if f in PAIRS else [cores[f]]
         pe.wait_ge(S["m%d" % f], sum(_count(s, workers, topo) for s in senders))
         for h in H:
             pe.wait_ge(S["vY" + h], t)
             pe.matmul(T["pt" + h][:, 0:64], T.tbl[:, 128 * f:128 * f + 128], T["oh" + h][:], True,
                       True).then_inc(S["pT" + h], 1)
+        if t == 2:
+            pe.wait_ge(S.cl2, 2)
         if t > 1:
             states(t - 1)
         if t == NT:
@@ -479,8 +493,8 @@ def _worker(g, core, r, cores, workers, T, topo):
             pe.wait_ge(S["vZ" + h], t)
             zh = z[:, 64 * a:64 * a + 64]
             if t < NT:
-                pe.matmul(T["py" + h][:, 0:64], T.ly[:], zh, True, True).then_inc(S["pY" + h], 1)
-                pe.matmul(T["px" + h][:, 0:64], T.lx[:], zh, True, True).then_inc(S["pX" + h], 1)
+                pe.matmul(T["py" + h][:, 0:64], ly[:], zh, True, True).then_inc(S["pY" + h], 1)
+                pe.matmul(T["px" + h][:, 0:64], lx[:], zh, True, True).then_inc(S["pX" + h], 1)
             else:
                 pe.matmul(T["py" + h][:, 0:64], T.one[:], zh, False, True).then_inc(S["pY" + h], 1)
         if t < NT:

from concourse.bass import DstId, RemoteDMATransfer
from concourse.mybir import AluOpType, ActivationFunctionType

N = 12
NW = 4
EB = 128
CB = EB // 16
LAST = N - 1
PAIRS = [5, 3]
SEQ = [f for f in range(LAST, 1, -1) if f + 1 not in PAIRS]
RES = [f - 2 if f in PAIRS else f - 1 for f in SEQ]
NT = len(SEQ)
WHOLE = {0: 1}
for _f in PAIRS:
    WHOLE[_f - 1] = _f
LISTERS = [11, 1, 6, 7]
BATCHES = [[1, 2, 3, 4], [5], [6], [7], [8]]
FIRST = {11: 0, 10: 512, 9: 1024, 8: 1024, 7: 1536, 6: 1536, 5: 0, 4: 1536, 3: 0, 2: 2048, 1: 0, 0: 8192}
NEXT = 1024
BIG = 16384.0
STD = (0x11F0, 0x0E0F)
TWO = (0x118E, 0x0E71)
SH = 2048

SCRATCH = {
    "raw": ("sbuf", [128, 64], "int32"),
    "raw8": ("sbuf", [128, 512], "int32"),
    "dws": ("dram", [128, 64], "int32"),
    "of1s": ("sbuf", [128, 512], "uint16"),
    "of1": ("sbuf", [128, 512], "uint16"),
    "two": ("sbuf", [128, 128], "int32"),
    "tb": ("sbuf", [128, 128], "float16"),
    "hls": ("sbuf", [128, 128], "uint16"),
    "st8": ("sbuf", [128, 32], "int32"),
    "off": ("sbuf", [128, 32], "uint16"),
    "win": ("sbuf", [128, 8192], "float32"),
    "win1": ("sbuf", [128, 8192], "float32"),
    "yy": ("sbuf", [128, 512], "float32"),
    "s4": ("sbuf", [128, 4], "int32"),
    "dw": ("dram", [128, 64], "int32"),
    "hl": ("sbuf", [128, 64], "uint16"),
    "row": ("sbuf", [128, 16], "int32"),
    "rowf": ("sbuf", [128, 16], "float32"),
    "w2": ("sbuf", [128, 16], "bfloat16"),
    "gs": ("sbuf", [128, 8], "float32"),
    "ox": ("sbuf", [128, 512], "bfloat16"),
    "zc": ("sbuf", [128, 512], "float32"),
    "cci": ("sbuf", [128, 32], "int32"),
    "tbl": ("sbuf", [128, N * 128], "float16"),
    "ip": ("sbuf", [128, 1], "int32"),
    "ic": ("sbuf", [128, 8], "int32"),
    "fc": ("sbuf", [128, 11], "float32"),
    "fd": ("sbuf", [128, 2], "float32"),
    "ci": ("sbuf", [128, 8], "int32"),
    "cf": ("sbuf", [128, 8], "float32"),
    "rr": ("sbuf", [128, 4, 64], "float16"),
    "sel": ("sbuf", [128, 2, 16], "bfloat16"),
    "onb": ("sbuf", [128, 128], "bfloat16"),
    "nul": ("sbuf", [128, 128], "bfloat16"),
    "lyb": ("sbuf", [128, 128], "bfloat16"),
    "lxb": ("sbuf", [128, 128], "bfloat16"),
    "one": ("sbuf", [128, 128], "float16"),
    "ly": ("sbuf", [128, 128], "float16"),
    "lx": ("sbuf", [128, 128], "float16"),
    "ly2": ("sbuf", [128, 128], "float16"),
    "lx2": ("sbuf", [128, 128], "float16"),
    "e16": ("sbuf", [16, 128], "bfloat16"),
    "bt": ("sbuf", [16, 128], "bfloat16"),
    "rs": ("sbuf", [128, 128], "float32"),
    "yc": ("sbuf", [128, 1], "float32"),
    "xc": ("sbuf", [128, 1], "float32"),
    "yc2": ("sbuf", [128, 1], "float32"),
    "xc2": ("sbuf", [128, 1], "float32"),
    "ohA": ("sbuf", [128, 64], "float16"),
    "ohB": ("sbuf", [128, 64], "float16"),
    "mxA": ("sbuf", [128, 64], "float16"),
    "mxB": ("sbuf", [128, 64], "float16"),
    "z0": ("sbuf", [128, 128], "float16"),
    "z1": ("sbuf", [128, 128], "float16"),
    "sc": ("sbuf", [128, NT * 128], "float32"),
    "offo": ("sbuf", [128, NT * CB], "uint16"),
    "ptA": ("psum", [128, 512], "float32"),
    "ptB": ("psum", [128, 512], "float32"),
    "pyA": ("psum", [128, 512], "float32"),
    "pyB": ("psum", [128, 512], "float32"),
    "pxA": ("psum", [128, 512], "float32"),
    "pxB": ("psum", [128, 512], "float32"),
    "po0": ("psum", [128, 512], "float32"),
    "po1": ("psum", [128, 512], "float32"),
}
SEMAPHORES = (["ld", "ld8", "ls", "prep", "prep8", "left", "left8", "leftl", "offin", "tab0", "tab1", "tab2", "tabin", "go",
               "stin", "st8in", "offok", "comp", "yv", "ya", "ys", "of1in", "dwin", "hlin", "wl", "k1", "k2", "k3", "oxs", "zs",
               "cs", "cbf", "cst", "chf", "cl2", "cip", "csel", "cbase", "cc1", "cc2", "cc3", "cc4", "ini", "iniY", "iniX",
               "pO", "vS0", "vS1", "vL", "gone"]
              + [k + h for k in ("pT", "pY", "pX", "vZ", "vY", "vX") for h in "AB"]
              + ["m%d" % f for f in SEQ] + ["cp%d" % b for b in range(len(BATCHES))])


def _bits(mask):
    return [1 << e for e in range(16) if (mask >> e) & 1]


def _split(mask, n):
    e = _bits(mask)
    k = len(e) // n
    return [sum(e[k * i:k * i + k]) for i in range(n)]


def _at(c, topo):
    return (topo.host(c), topo.chip(c))


def _workers(cores, topo):
    used = {_at(c, topo) for c in cores}
    got = {True: [], False: []}
    for c in range(256):
        if _at(c, topo) in used or topo.die(c) != topo.die(cores[0]):
            continue
        if not all(topo.may_write(c, d) and topo.may_write(d, c) for d in cores):
            continue
        k = topo.same_plane(c, cores[0])
        if len(got[k]) < NW // 2:
            got[k].append(c)
            used.add(_at(c, topo))
    return got[True] + got[False]


def _helpers(f, cores, workers, topo):
    own = cores[f - 1]
    got = [c for c in range(256) if c != own and _at(c, topo) == _at(own, topo)
           and all(topo.may_write(c, w) for w in workers) and topo.may_write(cores[f], c)]
    got.sort(key=lambda c: topo.die(c) != topo.die(own))
    return got[:2]


def _common(srcs_dsts, topo):
    m = 0xFFFF
    for s, d in srcs_dsts:
        m &= topo.mask(s, d)
    return m


def _count(src, dsts, topo):
    return len(_bits(_common([(src, d) for d in dsts], topo)))


def _dst(d, core, topo):
    rid, pid = topo.addr(d, core)
    return DstId(rid=rid, pnc=pid)


def _takers(t):
    b = RES[t - 1]
    return [b] + [r for r in sorted(WHOLE) if WHOLE[r] == b]


def _codes(k):
    return TWO if k + 1 < NT and SEQ[k + 1] in PAIRS else STD


def _batch_masks(b, w, cores, topo):
    m = _common([(w, cores[f]) for t in BATCHES[b] for f in _takers(t)], topo)
    return _split(m, len(BATCHES[b]))


def _send(g, core, src, dst, to, sem, left, topo):
    mask = _common([(core, c) for c in to], topo)
    g.remote_dma_fused([RemoteDMATransfer(dst_ids=[_dst(c, core, topo) for c in to], dma_engine_mask=mask,
                                          remote_sem=sem, srcs=[src], dsts=[dst for c in to])], local_sem=left)
    return len(_bits(mask))


def rank_program(g, core, T, topo):
    cores = list(T.cores)
    workers = _workers(cores, topo)
    rank = T.rank_of(core)
    if rank is not None:
        _rank(g, core, rank, cores, workers, T, topo)
    elif core in workers:
        _worker(g, core, workers.index(core), cores, workers, T, topo)
    else:
        for f in PAIRS:
            hs = _helpers(f, cores, workers, topo)
            if core in hs:
                _helper(g, core, f, hs.index(core), cores, workers, T, topo)


def _encode(v, src, n, masks, T, sem):
    for k in range(2):
        v.tensor_scalar(out=T.two[:, n * k:n * k + n], in0=src, scalar1=masks[k], scalar2=None,
                        op0=AluOpType.bitwise_and).then_inc(sem, 1)
    v.wait_ge(sem, 2)
    v.tensor_scalar(out=T.tb[:, 0:2 * n], in0=T.two[:, 0:2 * n], scalar1=-float(SH), scalar2=None,
                    op0=AluOpType.add).then_inc(sem, 1)


def _rank(g, core, f, cores, workers, T, topo):
    v, act, sync, S = g.vector, g.scalar, g.sync, T.sem
    first = FIRST[f]
    source = f in WHOLE.values()
    taken = f + 1 in PAIRS
    lister = f in LISTERS

    if lister:
        sync.dma_start(out=T.s4[:], in_=T.st[:]).then_inc(S.ls, 16)
    if taken:
        sync.dma_start(out=T.dws[:], in_=T.bp[:]).then_inc(S.ld, 16)
    elif f > 1:
        for a, q in enumerate((sync, act)):
            q.dma_start(out=T.raw[:, 32 * a:32 * a + 32], in_=T.bp[:, 256 * a:256 * a + 256]).then_inc(S.ld, 16)
    if source:
        for b in range(8):
            q = sync if b % 2 == 0 else act
            q.dma_start(out=T.raw8[16 * b:16 * b + 16, :], in_=T.bp[:]).then_inc(S.ld8, 16)
    if lister:
        g.wait_ge(S.ls, 16)
        nl = _send(g, core, T.s4[:], T.s4[:], [workers[LISTERS.index(f)]], S.stin, S.leftl, topo)
        sync.wait_ge(S.leftl, nl)
    if first:
        sync.dma_start(out=T.win[:, 0:first], in_=T.tab[:, 0:first]).then_inc(S.tab0, 16)

    ne = 0
    rest = first
    if taken:
        g.wait_ge(S.ld, 16)
        ne = _send(g, core, T.dws[:], T.dw[:], _helpers(f + 1, cores, workers, topo), S.dwin, S.left, topo)
        g.sem_inc(S.go, 1)
        for gate, n, done in ((S.go, 1, S.tab1), (S.tab0, 16, S.tab2)):
            sync.wait_ge(gate, n)
            sync.dma_start(out=T.win[:, rest:rest + NEXT], in_=T.tab[:, rest:rest + NEXT]).then_inc(done, 16)
            rest += NEXT
    elif f in PAIRS:
        v.wait_ge(S.ld, 32)
        for a in range(2):
            for k, (op, c) in enumerate(((AluOpType.logical_shift_right, 4), (AluOpType.bitwise_and, 15))):
                v.tensor_scalar(out=T.two[:, 64 * a + 32 * k:64 * a + 32 * k + 32], in0=T.raw[:, 32 * a:32 * a + 32],
                                scalar1=c, scalar2=None, op0=op).then_inc(S.prep, 1)
        v.wait_ge(S.prep, 4)
        v.tensor_copy(out=T.hls[:], in_=T.two[:]).then_inc(S.prep, 1)
        hs = _helpers(f, cores, workers, topo)
        m = _common([(core, h) for h in hs], topo)
        g.wait_ge(S.prep, 5)
        g.remote_dma_fused([RemoteDMATransfer(dst_ids=[_dst(h, core, topo)], dma_engine_mask=mm, remote_sem=S.hlin,
                                              srcs=[T.hls[:, 64 * a:64 * a + 64]], dsts=[T.hl[:]])
                            for a, (h, mm) in enumerate(zip(hs, _split(m, 2)))], local_sem=S.left)
        ne = len(_bits(m))
    elif f > 1:
        v.wait_ge(S.ld, 32)
        _encode(v, T.raw[:], 64, _codes(SEQ.index(f)), T, S.prep)
        g.wait_ge(S.prep, 3)
        if first:
            g.wait_ge(S.tab0, 16)
        ne = _send(g, core, T.tb[:], T.tbl[:, 128 * f:128 * f + 128], workers, S["m%d" % f], S.left, topo)
    n8 = 0
    if source:
        v.wait_ge(S.ld8, 128)
        v.tensor_copy(out=T.of1s[:], in_=T.raw8[:]).then_inc(S.prep8, 1)
        g.wait_ge(S.prep8, 1)
        n8 = _send(g, core, T.of1s[:], T.of1[:], [cores[f - 1]], S.of1in, S.left8, topo)

    if rest < 8192:
        if ne:
            sync.wait_ge(S.left, ne)
        if n8:
            sync.wait_ge(S.left8, n8)
        sync.dma_start(out=T.win[:, rest:8192], in_=T.tab[:, rest:8192]).then_inc(S.tabin, 16)

    def tab_there(q):
        if first:
            q.wait_ge(S.tab0, 16)
        if taken:
            q.wait_ge(S.tab1, 16)
            q.wait_ge(S.tab2, 16)
        if rest < 8192:
            q.wait_ge(S.tabin, 16)

    if f == LAST:
        for b in range(8):
            act.dma_start(out=T.st8[16 * b:16 * b + 16, :], in_=T.st[:]).then_inc(S.st8in, 16)
        v.wait_ge(S.st8in, 128)
        v.tensor_copy(out=T.off[:], in_=T.st8[:]).then_inc(S.offok, 1)
        osem, on = S.offok, 1
    else:
        osem, on = S.offin, 0
        for w in workers:
            for b, steps in enumerate(BATCHES):
                for t, mm in zip(steps, _batch_masks(b, w, cores, topo)):
                    if f in _takers(t):
                        on += len(_bits(mm))

    win = T.win
    tab_there(v)
    tab_there(act)
    if f in WHOLE:
        n1 = _count(cores[f + 1], [core], topo)
        win = T.win1
        v.wait_ge(S.of1in, n1)
        v.tensor_copy(out=win[:, 0:4096], in_=T.win[:].indirect(T.of1[:, 0:256])).then_inc(S.comp, 1)
        act.wait_ge(S.of1in, n1)
        act.activation(out=win[:, 4096:8192], in_=T.win[:].indirect(T.of1[:, 256:512]),
                       func=ActivationFunctionType.Copy, bias=-0.0).then_inc(S.comp, 1)
        v.wait_ge(S.comp, 2)
        act.wait_ge(S.comp, 2)
    v.wait_ge(osem, on)
    v.tensor_copy(out=T.yy[:, 0:256], in_=win[:].indirect(T.off[:, 0:16])).then_inc(S.yv, 1)
    act.wait_ge(osem, on)
    act.activation(out=T.yy[:, 256:512], in_=win[:].indirect(T.off[:, 16:32]),
                   func=ActivationFunctionType.Copy, bias=-0.0).then_inc(S.ya, 1)
    sync.wait_ge(S.yv, 1)
    sync.dma_start(out=T.y[:, 0:256], in_=T.yy[:, 0:256]).then_inc(S.ys, 16)
    act.wait_ge(S.ya, 1)
    act.dma_start(out=T.y[:, 256:512], in_=T.yy[:, 256:512]).then_inc(S.ys, 16)
    sync.wait_ge(S.ys, 32)


def _helper(g, core, f, m, cores, workers, T, topo):
    v, act, pe, sync, S = g.vector, g.scalar, g.tensor, g.sync, T.sem
    eq, mult = AluOpType.is_equal, AluOpType.mult
    g.iota(T.ip[:], [[0, 1]], 0, 1).then_inc(S.cip, 1)
    g.iota(T.row[:], [[1, 16]], 0, 0).then_inc(S.cip, 1)
    v.wait_ge(S.cip, 2)
    v.tensor_scalar(out=T.ic[:, 0:1], in0=T.ip[:], scalar1=15, scalar2=None, op0=AluOpType.bitwise_and).then_inc(S.k1, 1)
    v.tensor_scalar(out=T.ic[:, 1:2], in0=T.ip[:], scalar1=4, scalar2=None,
                    op0=AluOpType.logical_shift_right).then_inc(S.k1, 1)
    v.tensor_copy(out=T.rowf[:], in_=T.row[:]).then_inc(S.k1, 1)
    v.wait_ge(S.k1, 3)
    v.tensor_copy(out=T.fc[:, 0:2], in_=T.ic[:, 0:2]).then_inc(S.k2, 1)
    v.wait_ge(S.k2, 1)
    v.tensor_scalar(out=T.w2[:], in0=T.rowf[:], scalar1=T.fc[:, 0:1], scalar2=None, op0=eq).then_inc(S.k3, 1)
    v.tensor_scalar(out=T.gs[:], in0=T.rowf[:, 0:8], scalar1=T.fc[:, 1:2], scalar2=None, op0=eq).then_inc(S.k3, 1)

    nd = _count(cores[f - 1], _helpers(f, cores, workers, topo), topo)
    for b in range(8):
        q = sync if b % 2 == 0 else act
        q.wait_ge(S.dwin, nd)
        q.dma_start(out=T.raw8[16 * b:16 * b + 16, :], in_=T.dw[:]).then_inc(S.wl, 16)

    nh = _count(cores[f], _helpers(f, cores, workers, topo), topo) // 2
    act.wait_ge(S.k3, 2)
    act.wait_ge(S.hlin, nh)
    v.wait_ge(S.hlin, nh)
    v.wait_ge(S.wl, 128)
    pe.wait_ge(S.k3, 2)
    for k in range(4):
        c = slice(128 * k, 128 * k + 128)
        act.activation(out=T.ox[:, c], in_=T.w2[:].indirect(T.hl[:, 32 + 8 * k:40 + 8 * k]),
                       func=ActivationFunctionType.Copy).then_inc(S.oxs, 1)
        v.wait_ge(S.oxs, k + 1)
        v.tensor_tensor(out=T.zc[:, c], in0=T.raw8[:].indirect(T.hl[:, 8 * k:8 * k + 8]), in1=T.ox[:, c],
                        op=mult).then_inc(S.zs, 1)
        pe.wait_ge(S.zs, k + 1)
        pe.matmul(T.ptA[:, 8 * k:8 * k + 8], T.zc[:, c], T.gs[:], True, True).then_inc(S.cs, 1)
    v.wait_ge(S.cs, 4)
    v.tensor_copy(out=T.cci[:], in_=T.ptA[:, 0:32]).then_inc(S.k2, 1)
    v.wait_ge(S.k2, 2)
    _encode(v, T.cci[:], 32, _codes(SEQ.index(f)), T, S.prep)
    g.wait_ge(S.prep, 3)
    ne = _send(g, core, T.tb[:, 0:64], T.tbl[:, 128 * f + 64 * m:128 * f + 64 * m + 64], workers, S["m%d" % f], S.left, topo)
    g.wait_ge(S.left, ne)


def _worker(g, core, r, cores, workers, T, topo):
    v, pe, S = g.vector, g.tensor, T.sem
    H = "AB"
    eq, mult, add = AluOpType.is_equal, AluOpType.mult, AluOpType.add
    band, shr = AluOpType.bitwise_and, AluOpType.logical_shift_right

    g.iota(T.ip[:], [[0, 1]], 0, 1).then_inc(S.cip, 1)
    v.memset(T.onb[:], 1.0).then_inc(S.cbf, 1)
    v.memset(T.nul[:], 2.0 * SH).then_inc(S.cbf, 1)
    g.wait_ge(S.cbf, 2)
    g.affine_select(T.sel[:, 0, :], T.onb[:, 0:16], [[8, 16]], eq, 0.0, 2 * r, -1).then_inc(S.csel, 1)
    g.affine_select(T.sel[:, 1, :], T.onb[:, 0:16], [[8, 16]], eq, 0.0, 2 * r + 1, -1).then_inc(S.csel, 1)
    g.affine_select(T.e16[:], T.onb[0:16, :], [[0, 8], [1, 16]], eq, 0.0, 0, -1).then_inc(S.cbase, 1)
    g.affine_select(T.bt[:], T.nul[0:16, :], [[0, 8], [1, 16]], eq, -BIG, 0, -1).then_inc(S.cbase, 1)

    fills = [(T.rs[:], 0.0),
             (T.lxb[0:64, :], 1.0), (T.lxb[64:128, :], 0.0),
             (T.lyb[0:64, :], 0.0), (T.lyb[64:128, :], 1.0)]
    for ap, c in fills:
        v.memset(ap, c).then_inc(S.cst, 1)
    v.wait_ge(S.cip, 1)
    bits = ((shr, 3), (band, 7), (band, 31), (band, 32), (band, 112), None, (band, 24), (shr, 6))
    for k, oc in enumerate(bits):
        if oc is None:
            v.tensor_scalar(out=T.ic[:, k:k + 1], in0=T.ip[:], scalar1=3, scalar2=1, op0=shr, op1=band).then_inc(S.cc1, 1)
        else:
            v.tensor_scalar(out=T.ic[:, k:k + 1], in0=T.ip[:], scalar1=oc[1], scalar2=None, op0=oc[0]).then_inc(S.cc1, 1)
    v.wait_ge(S.cc1, 8)
    sh = -float(SH)
    lin = ((0, 1.0, 0.0), (1, 512.0, sh), (2, 16.0, sh), (3, 128.0, 0.0), (4, 1.0, 0.0), (5, 1.0, 0.0), (6, 16.0, 0.0),
           (7, 4096.0, 0.0), (1, 2.0, sh), (3, 0.03125, 0.0), (3, -0.03125, 1.0))
    for k, (j, m, a) in enumerate(lin):
        v.tensor_scalar(out=T.fc[:, k:k + 1], in0=T.ic[:, j:j + 1], scalar1=m, scalar2=a, op0=mult,
                        op1=add).then_inc(S.cc2, 1)
    v.wait_ge(S.cc2, len(lin))
    for o, p, q in ((T.yc[:], 0, 1), (T.xc[:], 2, 3), (T.fd[:, 0:1], 4, 5), (T.fd[:, 1:2], 6, 7)):
        v.tensor_tensor(out=o, in0=T.fc[:, p:p + 1], in1=T.fc[:, q:q + 1], op=add).then_inc(S.cc3, 1)
    v.wait_ge(S.cbf, 2)
    v.wait_ge(S.cst, len(fills))
    v.tensor_copy(out=T.one[:], in_=T.onb[:]).then_inc(S.chf, 1)
    v.tensor_copy(out=T.ly[:], in_=T.lyb[:]).then_inc(S.chf, 1)
    v.tensor_copy(out=T.lx[:], in_=T.lxb[:]).then_inc(S.chf, 1)
    v.memset(T.rs[:, 0:128:16], -2 * BIG).then_inc(S.chf, 1)
    v.wait_ge(S.cc3, 4)
    v.tensor_tensor(out=T.yc2[:], in0=T.fd[:, 0:1], in1=T.fc[:, 1:2], op=add).then_inc(S.cc4, 1)
    v.tensor_tensor(out=T.xc2[:], in0=T.fd[:, 1:2], in1=T.fc[:, 8:9], op=add).then_inc(S.cc4, 1)

    v.wait_ge(S.cc4, 2)
    v.wait_ge(S.chf, 4)
    v.wait_ge(S.csel, 2)
    pe.wait_ge(S.chf, 4)
    v.wait_ge(S.stin, _count(cores[LISTERS[r]], [core], topo))
    v.tensor_scalar(out=T.ci[:, 0:4], in0=T.s4[:], scalar1=STD[0], scalar2=None, op0=band).then_inc(S.ini, 1)
    v.tensor_scalar(out=T.ci[:, 4:8], in0=T.s4[:], scalar1=STD[1], scalar2=None, op0=band).then_inc(S.ini, 1)
    v.wait_ge(S.ini, 2)
    v.tensor_scalar(out=T.cf[:], in0=T.ci[:], scalar1=-float(SH), scalar2=None, op0=add).then_inc(S.ini, 1)
    v.wait_ge(S.ini, 3)
    for k, q in ((1, "Y"), (0, "X")):
        for l in range(4):
            v.tensor_scalar(out=T.rr[:, 2 * k:2 * k + 2, 16 * l:16 * l + 16], in0=T.sel[:],
                            scalar1=T.cf[:, 4 * k + l:4 * k + l + 1], scalar2=None, op0=mult).then_inc(S["ini" + q], 1)
    pe.wait_ge(S.iniY, 4)
    for a, h in enumerate(H):
        pe.matmul(T["py" + h][:, 0:64], T.one[:], T.rr[:, 2 + a, :], True, True).then_inc(S["pY" + h], 1)
    pe.wait_ge(S.iniX, 4)
    for a, h in enumerate(H):
        pe.matmul(T["px" + h][:, 0:64], T.one[:], T.rr[:, a, :], True, True).then_inc(S["pX" + h], 1)

    def onehots(h, n):
        yc, xc = (T.yc2, T.xc2) if SEQ[n - 1] in PAIRS else (T.yc, T.xc)
        v.wait_ge(S["pY" + h], n)
        v.tensor_scalar(out=T["oh" + h][:], in0=T["py" + h][:, 0:64], scalar1=yc[:, 0:1], scalar2=None,
                        op0=eq).then_inc(S["vY" + h], 1)
        v.wait_ge(S["pX" + h], n)
        v.tensor_scalar(out=T["mx" + h][:], in0=T["px" + h][:, 0:64], scalar1=xc[:, 0:1], scalar2=None,
                        op0=eq).then_inc(S["vX" + h], 1)

    nscan = [0, 0]

    def scan(t):
        v.wait_ge(S.pO, t)
        v.tensor_tensor_scan(T.sc[:, 128 * (t - 1):128 * t], T.rs[:], T["po%d" % (t % 2)][:, 0:128], 0.0,
                             add, AluOpType.max).then_inc(S["vS%d" % (t % 2)], 1)
        nscan[t % 2] += 1

    def pack(t):
        for b, steps in enumerate(BATCHES):
            if steps[-1] == t:
                for k in range(2):
                    if nscan[k]:
                        v.wait_ge(S["vS%d" % k], nscan[k])
                if t == NT:
                    v.wait_ge(S.vL, 2)
                t0 = steps[0] - 1
                v.tensor_copy(out=T.offo[:, CB * t0:CB * t],
                              in_=T.sc[:, 128 * t0 + 15:128 * t:16]).then_inc(S["cp%d" % b], 1)

    def base(t):
        k = t % 2
        before = len([u for u in range(1, t) if u % 2 == k])
        if before:
            pe.wait_ge(S["vS%d" % k], before)
        else:
            pe.wait_ge(S.cbase, 2)
        pe.matmul(T["po%d" % k][:, 0:128], T.e16[:], T.bt[:], True, False)

    def states(t):
        pe.matmul(T["po%d" % (t % 2)][:, 0:128], T.one[:], T["z%d" % (t % 2)][:], False, True).then_inc(S.pO, 1)

    for h in H:
        onehots(h, 1)
    v.tensor_scalar(out=T.ly2[:], in0=T.onb[:], scalar1=T.fc[:, 9:10], scalar2=None, op0=mult).then_inc(S.cl2, 1)
    v.tensor_scalar(out=T.lx2[:], in0=T.onb[:], scalar1=T.fc[:, 10:11], scalar2=None, op0=mult).then_inc(S.cl2, 1)
    for t in range(1, NT + 1):
        f = SEQ[t - 1]
        z = T["z%d" % (t % 2)]
        ly, lx = (T.ly2, T.lx2) if f in PAIRS else (T.ly, T.lx)
        senders = _helpers(f, cores, workers, topo) if f in PAIRS else [cores[f]]
        pe.wait_ge(S["m%d" % f], sum(_count(s, workers, topo) for s in senders))
        for h in H:
            pe.wait_ge(S["vY" + h], t)
            pe.matmul(T["pt" + h][:, 0:64], T.tbl[:, 128 * f:128 * f + 128], T["oh" + h][:], True,
                      True).then_inc(S["pT" + h], 1)
        if t == 2:
            pe.wait_ge(S.cl2, 2)
        if t > 1:
            states(t - 1)
        if t == NT:
            for h in H:
                pe.matmul(T["py" + h][:, 0:64], T.e16[:], T.bt[:, 0:64], True, False)
        for a, h in enumerate(H):
            pe.wait_ge(S["vZ" + h], t)
            zh = z[:, 64 * a:64 * a + 64]
            if t < NT:
                pe.matmul(T["py" + h][:, 0:64], ly[:], zh, True, True).then_inc(S["pY" + h], 1)
                pe.matmul(T["px" + h][:, 0:64], lx[:], zh, True, True).then_inc(S["pX" + h], 1)
            else:
                pe.matmul(T["py" + h][:, 0:64], T.one[:], zh, False, True).then_inc(S["pY" + h], 1)
        if t < NT:
            base(t)
        for a, h in enumerate(H):
            v.wait_ge(S["vX" + h], t)
            v.wait_ge(S["pT" + h], t)
            v.tensor_tensor(out=z[:, 64 * a:64 * a + 64], in0=T["pt" + h][:, 0:64], in1=T["mx" + h][:],
                            op=mult).then_inc(S["vZ" + h], 1)
        if t > 1:
            scan(t - 1)
        if t < NT:
            onehots("A", t + 1)
            pack(t - 1)
            onehots("B", t + 1)
        else:
            pack(t - 1)
            for a, h in enumerate(H):
                v.wait_ge(S["pY" + h], NT + 1)
                c = 128 * (NT - 1) + 64 * a
                v.tensor_tensor_scan(T.sc[:, c:c + 64], T.rs[:, 0:64], T["py" + h][:, 0:64], 0.0,
                                     add, AluOpType.max).then_inc(S.vL, 1)
            pack(t)

    total = 0
    for b, steps in enumerate(BATCHES):
        masks = _batch_masks(b, core, cores, topo)
        g.wait_ge(S["cp%d" % b], 1)
        g.remote_dma_fused([RemoteDMATransfer(dst_ids=[_dst(cores[f], core, topo) for f in _takers(t)],
                                              dma_engine_mask=mm, remote_sem=S.offin,
                                              srcs=[T.offo[:, CB * (t - 1):CB * t]],
                                              dsts=[T.off[:, CB * r:CB * r + CB] for f in _takers(t)])
                            for t, mm in zip(steps, masks)], local_sem=S.gone)
        total += sum(len(_bits(mm)) for mm in masks)
    g.wait_ge(S.gone, total)
